import numpy as np
import ml_dtypes


def mxq(x, axis, fmt="e4m3"):
    dtype, down = {"e4m3": (ml_dtypes.float8_e4m3fn, 7), "e5m2": (ml_dtypes.float8_e5m2, 14)}[fmt]
    v = np.moveaxis(np.asarray(x, np.float32).astype(ml_dtypes.bfloat16).astype(np.float64), axis, -1)
    blocks = v.reshape(v.shape[:-1] + (-1, 32))
    amax = np.abs(blocks).max(-1, keepdims=True)
    byte = np.maximum(np.where(amax > 0, np.frexp(amax)[1] - 1 + 127, 0) - down, 1)
    scale = np.exp2(byte - 127.0)
    codes = (blocks / scale).astype(np.float32).astype(dtype).astype(np.float64)
    return np.moveaxis((codes * scale).reshape(v.shape), -1, axis)


WIDE = False


def mx_kscale(k):
    if not WIDE:
        return np.ones(k)
    levels = np.array([30, -30])
    if k % 512:
        return np.exp2(np.random.permutation(np.resize(levels, k // 32))).repeat(32)
    a = np.empty((k // 512, 16))
    for p in range(k // 512):
        a[p, :8] = np.random.permutation(np.resize(levels, 8))
        for g in range(8):
            far = levels[np.abs(levels - a[p, g]) >= 10]
            a[p, g + 8] = far[np.random.randint(len(far))]
    return np.exp2(a.ravel()).repeat(32)


def f64(x):
    return np.asarray(x).astype(np.float64)


E2M1 = np.array([0.0, 0.5, 1.0, 1.5, 2.0, 3.0, 4.0, 6.0, -0.0, -0.5, -1.0, -1.5, -2.0, -3.0, -4.0, -6.0])


def pack_weight(w, fmt):
    k, n = w.shape
    w = f64(np.asarray(w, np.float32).astype(ml_dtypes.bfloat16)).reshape(k // 32, 32, n)
    amax = np.abs(w).max(1)
    if fmt == "e4m3":
        byte = np.frexp(amax)[1] - 1 + 127 - 7
    else:
        mant, ex = np.frexp(amax / 6.0)
        byte = np.where(mant > 0.5, ex, ex - 1) + 127
    byte = np.clip(np.where(amax > 0, byte, 1), 1, 254)
    scaled = (w * np.exp2(127.0 - byte)[:, None, :]).reshape(k, n).astype(np.float32)
    by_word = np.ascontiguousarray(scaled.reshape(k // 512, 128, 4, n).transpose(0, 1, 3, 2))
    if fmt == "e4m3":
        words = by_word.astype(ml_dtypes.float8_e4m3fn).view(np.uint8)
    else:
        c = by_word.astype(ml_dtypes.float4_e2m1fn).view(np.uint8) & 0xF
        words = (c[..., 0::2] | (c[..., 1::2] << 4)).reshape(k // 512, 128, 2 * n)
    return np.ascontiguousarray(words), np.ascontiguousarray(byte.astype(np.uint8).reshape(k // 512, 16, n))


def unpack_weight(words, scales, fmt):
    g, _, n = scales.shape
    words = np.ascontiguousarray(words).reshape(g, 128, n, -1)
    if fmt == "e4m3":
        vals = words.view(ml_dtypes.float8_e4m3fn).astype(np.float64)
    else:
        nib = np.empty((g, 128, n, 4), np.uint8)
        nib[..., 0::2] = words & 0xF
        nib[..., 1::2] = words >> 4
        vals = E2M1[nib]
    vals = vals * np.repeat(np.exp2(scales.astype(np.float64) - 127.0), 8, axis=1)[..., None]
    return vals.transpose(0, 1, 3, 2).reshape(g * 512, n)


N, R, K, T = 512, 512, 1024, 1536


def setup_inputs():
    n = np.random.standard_normal
    s = mx_kscale(N)[:, None]
    u = mx_kscale(R)[:, None]
    m = np.exp(0.5 * n((1, T)))
    p_w4 = pack_weight(n((N, K)) / np.sqrt(N) / s, "e2m1")
    return {
        "dy": (m * n((N, T)) * s).astype(np.float32),
        "w4_words": p_w4[0],
        "w4_scales": p_w4[1],
        "bu": (n((N, R)) / np.sqrt(N) / s * u.T).astype(np.float32),
        "ad": (0.5 * n((R, K)) / np.sqrt(R) / u).astype(np.float32),
    }


def reference(dy, w4_words, w4_scales, bu, ad):
    dy_ = mxq(f64(dy), 0, "e5m2")
    w4_ = unpack_weight(w4_words, w4_scales, "e2m1")
    bu_ = mxq(f64(bu), 0, "e4m3")
    h = bu_.T @ dy_
    h_ = mxq(h, 0, "e5m2")
    ad_ = mxq(f64(ad), 0, "e4m3")
    dx = w4_.T @ dy_ + ad_.T @ h_
    return dx, h

@@ -1,0 +1,192 @@
+from contextlib import ExitStack
+
+import concourse.mybir as mybir
+
+N, R, K, T = 512, 512, 1024, 1536
+FLOPS = 2 * N * R * T + 2 * (N + R) * K * T
+
+F32 = mybir.dt.float32
+BF16 = mybir.dt.bfloat16
+I32 = mybir.dt.int32
+U32 = mybir.dt.uint32
+U8 = mybir.dt.uint8
+E4M3 = mybir.dt.float8_e4m3fn_x4
+E5M2 = mybir.dt.float8_e5m2_x4
+E2M1 = mybir.dt.float4_e2m1fn_x4
+
+P = 128
+PACK = 4
+W = 512
+HALF = W // 2
+CHUNKS = T // W
+K_TILES = K // P
+BANKS = 8
+GROUP = W // P
+AHEAD = 6
+
+
+def tile_mix_lrbwd_none_kernel(tc, dy, w4_words, w4_scales, bu, ad, out_0, out_1):
+    nc = tc.nc
+    with ExitStack() as ctx:
+        sb = ctx.enter_context(tc.tile_pool(name="sb", bufs=1))
+        ps = ctx.enter_context(tc.psum_pool(name="ps", bufs=1))
+        ctx.enter_context(tc.manual_schedule())
+
+        def operand(name):
+            grouped = sb.tile([P, W * PACK], BF16, name=name + "_bf", align_bytes=64)
+            codes = sb.tile([P, W], U32, name=name + "_codes", align_bytes=64)
+            scales = sb.tile([P, W], U8, name=name + "_scales", align_bytes=64)
+            return grouped, codes, scales
+
+        def copy(engine, out, in_):
+            if engine == "vector":
+                nc.vector.tensor_copy(out=out, in_=in_)
+            else:
+                nc.scalar.copy(out=out, in_=in_)
+
+        def interleave(engine, op, raw, half):
+            src = raw[:, :, half * HALF : (half + 1) * HALF].rearrange("p j (c i) -> p c j i", i=4)
+            dst = op[0][:, half * HALF * PACK : (half + 1) * HALF * PACK].rearrange(
+                "p (c i j) -> p c j i", i=4, j=PACK
+            )
+            copy(engine, dst, src)
+
+        def quantize(op, fmt, half):
+            grouped, codes, scales = op
+            cols = slice(half * HALF, (half + 1) * HALF)
+            nc.vector.quantize_mx(
+                out=codes[:, cols].bitcast(fmt),
+                scales=scales[:, cols],
+                in_=grouped[:, half * HALF * PACK : (half + 1) * HALF * PACK],
+            )
+
+        def prepare(op, raw, fmt, second="vector"):
+            interleave("vector", op, raw, 0)
+            interleave(second, op, raw, 1)
+            quantize(op, fmt, 0)
+            quantize(op, fmt, 1)
+
+        banks_used = []
+
+        def bank():
+            i = len(banks_used) % BANKS
+            banks_used.append(i)
+            return ps.tile([P, W], F32, name="acc", tag="bank%d" % i)
+
+        dy_v = dy.rearrange("(p j) t -> p j t", j=PACK)
+        ad_v = ad.rearrange("(p j) k -> p j k", j=PACK)
+        dy_raw = [sb.tile([P, PACK, W], F32, name="dy_raw%d" % c) for c in range(CHUNKS)]
+        ad_raw = [sb.tile([P, PACK, W], F32, name="ad_raw%d" % a) for a in range(K // W)]
+        bu_raw = sb.tile([P, PACK, R], F32)
+        w4_codes = sb.tile([P, 2 * K], U8, align_bytes=64)
+        w4_plane = sb.tile([P, K], U8, align_bytes=64)
+
+        nc.gpsimd.memset(w4_plane[:].bitcast(I32), 0)
+        nc.sync.dma_start(out=dy_raw[0][:], in_=dy_v[:, :, 0:W])
+        nc.sync.dma_start(out=bu_raw[:], in_=bu.rearrange("(p j) r -> p j r", j=PACK))
+        for q in range(4):
+            nc.gpsimd.dma_start(
+                out=w4_plane[32 * q : 32 * q + 4, :].bitcast(I32),
+                in_=w4_scales[0, 4 * q : 4 * q + 4, :].bitcast(I32),
+            )
+        for c in range(1, CHUNKS):
+            nc.sync.dma_start(out=dy_raw[c][:], in_=dy_v[:, :, c * W : (c + 1) * W])
+        nc.sync.dma_start(out=w4_codes[:].bitcast(I32), in_=w4_words[0].bitcast(I32))
+        nc.sync.dma_start(out=ad_raw[0][:], in_=ad_v[:, :, 0:W])
+        nc.sync.dma_start(out=ad_raw[1][:], in_=ad_v[:, :, W : 2 * W])
+
+        dy_q = [operand("dy%d" % c) for c in range(CHUNKS)]
+        h_q = [operand("h%d" % c) for c in range(CHUNKS)]
+        ad_q = [operand("ad%d" % a) for a in range(K // W)]
+        bu_q = operand("bu")
+        h_sb = [sb.tile([P, PACK, W], F32, name="h_sb%d" % c) for c in range(CHUNKS)]
+        dx_sb = [
+            [sb.tile([P, GROUP, W], F32, name="dx_sb%d_%d" % (a, c)) for c in range(CHUNKS)] for a in range(K // W)
+        ]
+        dx_out = out_0.rearrange("(g p) t -> p g t", p=P)
+        h_out = out_1.rearrange("(p j) t -> p j t", j=PACK)
+
+        def prepare_bu():
+            dst = bu_q[0][:].rearrange("p (s m j) -> p m j s", s=PACK, j=PACK)
+            src = bu_raw[:].rearrange("p j (m s) -> p m j s", s=PACK)
+            nc.vector.tensor_copy(out=dst[:, 0:80], in_=src[:, 0:80])
+            nc.scalar.copy(out=dst[:, 80:128], in_=src[:, 80:128])
+            quantize(bu_q, E4M3, 0)
+            quantize(bu_q, E4M3, 1)
+
+        def h_chunk(c):
+            for j in range(PACK):
+                acc = bank()
+                cols = slice(j * P, (j + 1) * P)
+                nc.tensor.matmul_mx(
+                    out=acc[:],
+                    lhsT=bu_q[1][:, cols].bitcast(E4M3),
+                    lhsT_scale=bu_q[2][:, cols],
+                    rhs=dy_q[c][1][:].bitcast(E5M2),
+                    rhs_scale=dy_q[c][2][:],
+                    start=True,
+                    stop=True,
+                )
+                nc.scalar.copy(out=h_sb[c][:, j, :], in_=acc[:])
+            nc.sync.dma_start(out=h_out[:, :, c * W : (c + 1) * W], in_=h_sb[c][:])
+
+        tiles = [(a, c, g) for a in range(K // W) for c in range(CHUNKS) for g in range(GROUP)]
+        open_banks = {}
+
+        def base_pass(i):
+            a, c, g = tiles[i]
+            k = a * GROUP + g
+            acc = bank()
+            open_banks[i] = acc
+            nc.tensor.matmul_mx(
+                out=acc[:],
+                lhsT=w4_codes[:, 2 * k * P : 2 * (k + 1) * P].bitcast(E2M1),
+                lhsT_scale=w4_plane[:, k * P : (k + 1) * P],
+                rhs=dy_q[c][1][:].bitcast(E5M2),
+                rhs_scale=dy_q[c][2][:],
+                start=True,
+                stop=False,
+            )
+
+        def adapter_pass(i):
+            a, c, g = tiles[i]
+            acc = open_banks[i]
+            cols = slice(g * P, (g + 1) * P)
+            nc.tensor.matmul_mx(
+                out=acc[:],
+                lhsT=ad_q[a][1][:, cols].bitcast(E4M3),
+                lhsT_scale=ad_q[a][2][:, cols],
+                rhs=h_q[c][1][:].bitcast(E5M2),
+                rhs_scale=h_q[c][2][:],
+                start=False,
+                stop=True,
+            )
+            engine = "vector" if a == 1 and i % 2 == 0 else "scalar"
+            copy(engine, dx_sb[a][c][:, g, :], acc[:])
+            per_store = 2 if i >= len(tiles) - GROUP else GROUP
+            if (g + 1) % per_store == 0:
+                g0 = g + 1 - per_store
+                nc.sync.dma_start(
+                    out=dx_out[:, a * GROUP + g0 : a * GROUP + g + 1, c * W : (c + 1) * W],
+                    in_=dx_sb[a][c][:, g0 : g + 1, :],
+                )
+
+        prepare(dy_q[0], dy_raw[0][:], E5M2, second="scalar")
+        prepare_bu()
+        h_chunk(0)
+        for c in range(1, CHUNKS):
+            prepare(dy_q[c], dy_raw[c][:], E5M2)
+            h_chunk(c)
+        for i in range(AHEAD):
+            base_pass(i)
+        prepare(h_q[0], h_sb[0][:], E5M2)
+        prepare(ad_q[0], ad_raw[0][:], E4M3)
+        for i, (a, c, g) in enumerate(tiles):
+            adapter_pass(i)
+            if i + AHEAD < len(tiles):
+                base_pass(i + AHEAD)
+            if a == 0 and g == 0:
+                if c + 1 < CHUNKS:
+                    prepare(h_q[c + 1], h_sb[c + 1][:], E5M2)
+                else:
+                    prepare(ad_q[1], ad_raw[1][:], E4M3)

@@ -22,7 +22,9 @@ CHUNKS = T // W
 K_TILES = K // P
 BANKS = 8
 GROUP = W // P
-AHEAD = 6
+DY_VECTOR = 344
+AHEAD = 4
+SHARED_FROM = 10
 
 
 def tile_mix_lrbwd_none_kernel(tc, dy, w4_words, w4_scales, bu, ad, out_0, out_1):
@@ -44,11 +46,9 @@ def tile_mix_lrbwd_none_kernel(tc, dy, w4_words, w4_scales, bu, ad, out_0, out_1
             else:
                 nc.scalar.copy(out=out, in_=in_)
 
-        def interleave(engine, op, raw, half):
-            src = raw[:, :, half * HALF : (half + 1) * HALF].rearrange("p j (c i) -> p c j i", i=4)
-            dst = op[0][:, half * HALF * PACK : (half + 1) * HALF * PACK].rearrange(
-                "p (c i j) -> p c j i", i=4, j=PACK
-            )
+        def interleave(engine, op, raw, lo, hi, at=0):
+            src = raw[:, :, at + lo : at + hi].rearrange("p j (c i) -> p c j i", i=4)
+            dst = op[0][:, lo * PACK : hi * PACK].rearrange("p (c i j) -> p c j i", i=4, j=PACK)
             copy(engine, dst, src)
 
         def quantize(op, fmt, half):
@@ -60,9 +60,9 @@ def tile_mix_lrbwd_none_kernel(tc, dy, w4_words, w4_scales, bu, ad, out_0, out_1
                 in_=grouped[:, half * HALF * PACK : (half + 1) * HALF * PACK],
             )
 
-        def prepare(op, raw, fmt, second="vector"):
-            interleave("vector", op, raw, 0)
-            interleave(second, op, raw, 1)
+        def prepare(op, raw, fmt, at=0):
+            interleave("vector", op, raw, 0, HALF, at)
+            interleave("vector", op, raw, HALF, W, at)
             quantize(op, fmt, 0)
             quantize(op, fmt, 1)
 
@@ -74,8 +74,8 @@ def tile_mix_lrbwd_none_kernel(tc, dy, w4_words, w4_scales, bu, ad, out_0, out_1
             return ps.tile([P, W], F32, name="acc", tag="bank%d" % i)
 
         dy_v = dy.rearrange("(p j) t -> p j t", j=PACK)
-        ad_v = ad.rearrange("(p j) k -> p j k", j=PACK)
         dy_raw = [sb.tile([P, PACK, W], F32, name="dy_raw%d" % c) for c in range(CHUNKS)]
+        ad_v = ad.rearrange("(p j) k -> p j k", j=PACK)
         ad_raw = [sb.tile([P, PACK, W], F32, name="ad_raw%d" % a) for a in range(K // W)]
         bu_raw = sb.tile([P, PACK, R], F32)
         w4_codes = sb.tile([P, 2 * K], U8, align_bytes=64)
@@ -92,17 +92,20 @@ def tile_mix_lrbwd_none_kernel(tc, dy, w4_words, w4_scales, bu, ad, out_0, out_1
         for c in range(1, CHUNKS):
             nc.sync.dma_start(out=dy_raw[c][:], in_=dy_v[:, :, c * W : (c + 1) * W])
         nc.sync.dma_start(out=w4_codes[:].bitcast(I32), in_=w4_words[0].bitcast(I32))
-        nc.sync.dma_start(out=ad_raw[0][:], in_=ad_v[:, :, 0:W])
-        nc.sync.dma_start(out=ad_raw[1][:], in_=ad_v[:, :, W : 2 * W])
+        for a in range(K // W):
+            nc.sync.dma_start(out=ad_raw[a][:], in_=ad_v[:, :, a * W : (a + 1) * W])
 
         dy_q = [operand("dy%d" % c) for c in range(CHUNKS)]
         h_q = [operand("h%d" % c) for c in range(CHUNKS)]
         ad_q = [operand("ad%d" % a) for a in range(K // W)]
         bu_q = operand("bu")
         h_sb = [sb.tile([P, PACK, W], F32, name="h_sb%d" % c) for c in range(CHUNKS)]
-        dx_sb = [
-            [sb.tile([P, GROUP, W], F32, name="dx_sb%d_%d" % (a, c)) for c in range(CHUNKS)] for a in range(K // W)
-        ]
+        stores = [(a, c, 1) for a in range(K // W) for c in range(CHUNKS)]
+        dx_sb = {}
+        for a, c0, n in stores:
+            staged = sb.tile([P, GROUP, n * W], F32, name="dx_sb%d_%d" % (a, c0))
+            for c in range(c0, c0 + n):
+                dx_sb[a, c] = (staged, c0, n)
         dx_out = out_0.rearrange("(g p) t -> p g t", p=P)
         h_out = out_1.rearrange("(p j) t -> p j t", j=PACK)
 
@@ -130,14 +133,11 @@ def tile_mix_lrbwd_none_kernel(tc, dy, w4_words, w4_scales, bu, ad, out_0, out_1
                 nc.scalar.copy(out=h_sb[c][:, j, :], in_=acc[:])
             nc.sync.dma_start(out=h_out[:, :, c * W : (c + 1) * W], in_=h_sb[c][:])
 
-        tiles = [(a, c, g) for a in range(K // W) for c in range(CHUNKS) for g in range(GROUP)]
         open_banks = {}
 
-        def base_pass(i):
-            a, c, g = tiles[i]
-            k = a * GROUP + g
+        def base_pass(k, c):
             acc = bank()
-            open_banks[i] = acc
+            open_banks[k, c] = acc
             nc.tensor.matmul_mx(
                 out=acc[:],
                 lhsT=w4_codes[:, 2 * k * P : 2 * (k + 1) * P].bitcast(E2M1),
@@ -148,12 +148,11 @@ def tile_mix_lrbwd_none_kernel(tc, dy, w4_words, w4_scales, bu, ad, out_0, out_1
                 stop=False,
             )
 
-        def adapter_pass(i):
-            a, c, g = tiles[i]
-            acc = open_banks[i]
+        def adapter_pass(k, c):
+            a, g = divmod(k, GROUP)
             cols = slice(g * P, (g + 1) * P)
             nc.tensor.matmul_mx(
-                out=acc[:],
+                out=open_banks[k, c][:],
                 lhsT=ad_q[a][1][:, cols].bitcast(E4M3),
                 lhsT_scale=ad_q[a][2][:, cols],
                 rhs=h_q[c][1][:].bitcast(E5M2),
@@ -161,32 +160,60 @@ def tile_mix_lrbwd_none_kernel(tc, dy, w4_words, w4_scales, bu, ad, out_0, out_1
                 start=False,
                 stop=True,
             )
-            engine = "vector" if a == 1 and i % 2 == 0 else "scalar"
-            copy(engine, dx_sb[a][c][:, g, :], acc[:])
-            per_store = 2 if i >= len(tiles) - GROUP else GROUP
-            if (g + 1) % per_store == 0:
-                g0 = g + 1 - per_store
+
+        def empty(engine, k, c):
+            a, g = divmod(k, GROUP)
+            staged, c0, n = dx_sb[a, c]
+            copy(engine, staged[:, g, (c - c0) * W : (c - c0 + 1) * W], open_banks[k, c][:])
+            if g == GROUP - 1 and c == c0 + n - 1:
                 nc.sync.dma_start(
-                    out=dx_out[:, a * GROUP + g0 : a * GROUP + g + 1, c * W : (c + 1) * W],
-                    in_=dx_sb[a][c][:, g0 : g + 1, :],
+                    out=dx_out[:, a * GROUP : (a + 1) * GROUP, c0 * W : (c0 + n) * W], in_=staged[:]
                 )
 
-        prepare(dy_q[0], dy_raw[0][:], E5M2, second="scalar")
+        def ad_interleave(n):
+            a, half = divmod(n, 2)
+            interleave("vector", ad_q[a], ad_raw[a][:], half * HALF, (half + 1) * HALF)
+
+        def ad_quantize(n):
+            a, half = divmod(n, 2)
+            quantize(ad_q[a], E4M3, half)
+
+        tiles = [(a * GROUP + g, c) for a in range(K // W) for c in range(CHUNKS) for g in range(GROUP)]
+
+        def dx_tiles(first, last):
+            for i in range(first, last):
+                adapter_pass(*tiles[i])
+                empty("vector" if i >= SHARED_FROM and i % 2 == 0 else "scalar", *tiles[i])
+                if i + AHEAD < len(tiles):
+                    base_pass(*tiles[i + AHEAD])
+
+        interleave("vector", dy_q[0], dy_raw[0][:], 0, HALF)
+        interleave("vector", dy_q[0], dy_raw[0][:], HALF, DY_VECTOR)
+        interleave("scalar", dy_q[0], dy_raw[0][:], DY_VECTOR, W)
+        quantize(dy_q[0], E5M2, 0)
+        quantize(dy_q[0], E5M2, 1)
         prepare_bu()
         h_chunk(0)
         for c in range(1, CHUNKS):
             prepare(dy_q[c], dy_raw[c][:], E5M2)
             h_chunk(c)
         for i in range(AHEAD):
-            base_pass(i)
-        prepare(h_q[0], h_sb[0][:], E5M2)
-        prepare(ad_q[0], ad_raw[0][:], E4M3)
-        for i, (a, c, g) in enumerate(tiles):
-            adapter_pass(i)
-            if i + AHEAD < len(tiles):
-                base_pass(i + AHEAD)
-            if a == 0 and g == 0:
-                if c + 1 < CHUNKS:
-                    prepare(h_q[c + 1], h_sb[c + 1][:], E5M2)
-                else:
-                    prepare(ad_q[1], ad_raw[1][:], E4M3)
+            base_pass(*tiles[i])
+        interleave("vector", h_q[0], h_sb[0][:], 0, HALF)
+        interleave("vector", h_q[0], h_sb[0][:], HALF, W)
+        ad_interleave(0)
+        quantize(h_q[0], E5M2, 0)
+        quantize(h_q[0], E5M2, 1)
+        ad_quantize(0)
+        ad_interleave(1)
+        dx_tiles(0, 2)
+        interleave("vector", h_q[1], h_sb[1][:], 0, HALF)
+        ad_quantize(1)
+        dx_tiles(2, 4)
+        interleave("vector", h_q[1], h_sb[1][:], HALF, W)
+        quantize(h_q[1], E5M2, 0)
+        quantize(h_q[1], E5M2, 1)
+        dx_tiles(4, 8)
+        prepare(h_q[2], h_sb[2][:], E5M2)
+        prepare(ad_q[1], ad_raw[1][:], E4M3)
+        dx_tiles(8, len(tiles))

@@ -23,8 +23,8 @@ K_TILES = K // P
 BANKS = 8
 GROUP = W // P
 DY_VECTOR = 344
-AHEAD = 4
-SHARED_FROM = 10
+SHARED_FROM = 3
+LAST_STORES = [2, 3, 4]
 
 
 def tile_mix_lrbwd_none_kernel(tc, dy, w4_words, w4_scales, bu, ad, out_0, out_1):
@@ -100,12 +100,8 @@ def tile_mix_lrbwd_none_kernel(tc, dy, w4_words, w4_scales, bu, ad, out_0, out_1
         ad_q = [operand("ad%d" % a) for a in range(K // W)]
         bu_q = operand("bu")
         h_sb = [sb.tile([P, PACK, W], F32, name="h_sb%d" % c) for c in range(CHUNKS)]
-        stores = [(a, c, 1) for a in range(K // W) for c in range(CHUNKS)]
-        dx_sb = {}
-        for a, c0, n in stores:
-            staged = sb.tile([P, GROUP, n * W], F32, name="dx_sb%d_%d" % (a, c0))
-            for c in range(c0, c0 + n):
-                dx_sb[a, c] = (staged, c0, n)
+        groups = [(0, 4, 0, 1), (0, 4, 1, 1), (4, 2, 0, 2), (6, 2, 0, 2), (0, 4, 2, 1), (4, 4, 2, 1)]
+        dx_sb = [sb.tile([P, nk, nch * W], F32, name="dx_sb%d" % n) for n, (k0, nk, c0, nch) in enumerate(groups)]
         dx_out = out_0.rearrange("(g p) t -> p g t", p=P)
         h_out = out_1.rearrange("(p j) t -> p j t", j=PACK)
 
@@ -161,15 +157,6 @@ def tile_mix_lrbwd_none_kernel(tc, dy, w4_words, w4_scales, bu, ad, out_0, out_1
                 stop=True,
             )
 
-        def empty(engine, k, c):
-            a, g = divmod(k, GROUP)
-            staged, c0, n = dx_sb[a, c]
-            copy(engine, staged[:, g, (c - c0) * W : (c - c0 + 1) * W], open_banks[k, c][:])
-            if g == GROUP - 1 and c == c0 + n - 1:
-                nc.sync.dma_start(
-                    out=dx_out[:, a * GROUP : (a + 1) * GROUP, c0 * W : (c0 + n) * W], in_=staged[:]
-                )
-
         def ad_interleave(n):
             a, half = divmod(n, 2)
             interleave("vector", ad_q[a], ad_raw[a][:], half * HALF, (half + 1) * HALF)
@@ -178,14 +165,27 @@ def tile_mix_lrbwd_none_kernel(tc, dy, w4_words, w4_scales, bu, ad, out_0, out_1
             a, half = divmod(n, 2)
             quantize(ad_q[a], E4M3, half)
 
-        tiles = [(a * GROUP + g, c) for a in range(K // W) for c in range(CHUNKS) for g in range(GROUP)]
+        def members(n):
+            k0, nk, c0, nch = groups[n]
+            return [(k, c) for k in range(k0, k0 + nk) for c in range(c0, c0 + nch)]
 
-        def dx_tiles(first, last):
+        def open_group(n):
+            for k, c in members(n):
+                base_pass(k, c)
+
+        def close_group(n, first=0, last=GROUP):
+            k0, nk, c0, nch = groups[n]
+            ends = LAST_STORES if n == len(groups) - 1 else [GROUP]
             for i in range(first, last):
-                adapter_pass(*tiles[i])
-                empty("vector" if i >= SHARED_FROM and i % 2 == 0 else "scalar", *tiles[i])
-                if i + AHEAD < len(tiles):
-                    base_pass(*tiles[i + AHEAD])
+                k, c = members(n)[i]
+                adapter_pass(k, c)
+                engine = "vector" if n >= SHARED_FROM and i % 2 == 0 else "scalar"
+                copy(engine, dx_sb[n][:, k - k0, (c - c0) * W : (c - c0 + 1) * W], open_banks[k, c][:])
+                if i + 1 in ends:
+                    g0 = ([0] + ends)[ends.index(i + 1)] // nch
+                    nc.sync.dma_start(
+                        out=dx_out[:, k0 + g0 : k + 1, c0 * W : (c0 + nch) * W], in_=dx_sb[n][:, g0 : k + 1 - k0, :]
+                    )
 
         interleave("vector", dy_q[0], dy_raw[0][:], 0, HALF)
         interleave("vector", dy_q[0], dy_raw[0][:], HALF, DY_VECTOR)
@@ -197,8 +197,7 @@ def tile_mix_lrbwd_none_kernel(tc, dy, w4_words, w4_scales, bu, ad, out_0, out_1
         for c in range(1, CHUNKS):
             prepare(dy_q[c], dy_raw[c][:], E5M2)
             h_chunk(c)
-        for i in range(AHEAD):
-            base_pass(*tiles[i])
+        open_group(0)
         interleave("vector", h_q[0], h_sb[0][:], 0, HALF)
         interleave("vector", h_q[0], h_sb[0][:], HALF, W)
         ad_interleave(0)
@@ -206,14 +205,24 @@ def tile_mix_lrbwd_none_kernel(tc, dy, w4_words, w4_scales, bu, ad, out_0, out_1
         quantize(h_q[0], E5M2, 1)
         ad_quantize(0)
         ad_interleave(1)
-        dx_tiles(0, 2)
+        interleave("scalar", h_q[1], h_sb[1][:], HALF, W)
+        close_group(0, 0, 2)
+        open_group(1)
         interleave("vector", h_q[1], h_sb[1][:], 0, HALF)
         ad_quantize(1)
-        dx_tiles(2, 4)
-        interleave("vector", h_q[1], h_sb[1][:], HALF, W)
+        close_group(0, 2, 4)
         quantize(h_q[1], E5M2, 0)
         quantize(h_q[1], E5M2, 1)
-        dx_tiles(4, 8)
+        close_group(1)
+        ad_interleave(2)
+        ad_interleave(3)
+        ad_quantize(2)
+        ad_quantize(3)
         prepare(h_q[2], h_sb[2][:], E5M2)
-        prepare(ad_q[1], ad_raw[1][:], E4M3)
-        dx_tiles(8, len(tiles))
+        for n in (2, 3):
+            open_group(n)
+            close_group(n)
+        open_group(4)
+        open_group(5)
+        close_group(4)
+        close_group(5)

@@ -24,7 +24,7 @@ BANKS = 8
 GROUP = W // P
 DY_VECTOR = 344
 SHARED_FROM = 3
-LAST_STORES = [2, 3, 4]
+LAST_STORES = [2, 4]
 
 
 def tile_mix_lrbwd_none_kernel(tc, dy, w4_words, w4_scales, bu, ad, out_0, out_1):
@@ -35,9 +35,9 @@ def tile_mix_lrbwd_none_kernel(tc, dy, w4_words, w4_scales, bu, ad, out_0, out_1
         ctx.enter_context(tc.manual_schedule())
 
         def operand(name):
-            grouped = sb.tile([P, W * PACK], BF16, name=name + "_bf", align_bytes=64)
-            codes = sb.tile([P, W], U32, name=name + "_codes", align_bytes=64)
-            scales = sb.tile([P, W], U8, name=name + "_scales", align_bytes=64)
+            grouped = sb.tile([P, W * PACK], BF16, name=name + "_bf", align_bytes=256)
+            codes = sb.tile([P, W], U32, name=name + "_codes", align_bytes=256)
+            scales = sb.tile([P, W], U8, name=name + "_scales", align_bytes=256)
             return grouped, codes, scales
 
         def copy(engine, out, in_):
@@ -74,12 +74,12 @@ def tile_mix_lrbwd_none_kernel(tc, dy, w4_words, w4_scales, bu, ad, out_0, out_1
             return ps.tile([P, W], F32, name="acc", tag="bank%d" % i)
 
         dy_v = dy.rearrange("(p j) t -> p j t", j=PACK)
-        dy_raw = [sb.tile([P, PACK, W], F32, name="dy_raw%d" % c) for c in range(CHUNKS)]
+        dy_raw = [sb.tile([P, PACK, W], F32, name="dy_raw%d" % c, align_bytes=256) for c in range(CHUNKS)]
         ad_v = ad.rearrange("(p j) k -> p j k", j=PACK)
-        ad_raw = [sb.tile([P, PACK, W], F32, name="ad_raw%d" % a) for a in range(K // W)]
-        bu_raw = sb.tile([P, PACK, R], F32)
-        w4_codes = sb.tile([P, 2 * K], U8, align_bytes=64)
-        w4_plane = sb.tile([P, K], U8, align_bytes=64)
+        ad_raw = [sb.tile([P, PACK, W], F32, name="ad_raw%d" % a, align_bytes=256) for a in range(K // W)]
+        bu_raw = sb.tile([P, PACK, R], F32, align_bytes=256)
+        w4_codes = sb.tile([P, 2 * K], U8, align_bytes=256)
+        w4_plane = sb.tile([P, K], U8, align_bytes=256)
 
         nc.gpsimd.memset(w4_plane[:].bitcast(I32), 0)
         nc.sync.dma_start(out=dy_raw[0][:], in_=dy_v[:, :, 0:W])
@@ -99,9 +99,9 @@ def tile_mix_lrbwd_none_kernel(tc, dy, w4_words, w4_scales, bu, ad, out_0, out_1
         h_q = [operand("h%d" % c) for c in range(CHUNKS)]
         ad_q = [operand("ad%d" % a) for a in range(K // W)]
         bu_q = operand("bu")
-        h_sb = [sb.tile([P, PACK, W], F32, name="h_sb%d" % c) for c in range(CHUNKS)]
+        h_sb = [sb.tile([P, PACK, W], F32, name="h_sb%d" % c, align_bytes=256) for c in range(CHUNKS)]
         groups = [(0, 4, 0, 1), (0, 4, 1, 1), (4, 2, 0, 2), (6, 2, 0, 2), (0, 4, 2, 1), (4, 4, 2, 1)]
-        dx_sb = [sb.tile([P, nk, nch * W], F32, name="dx_sb%d" % n) for n, (k0, nk, c0, nch) in enumerate(groups)]
+        dx_sb = [sb.tile([P, nk, nch * W], F32, name="dx_sb%d" % n, align_bytes=256) for n, (k0, nk, c0, nch) in enumerate(groups)]
         dx_out = out_0.rearrange("(g p) t -> p g t", p=P)
         h_out = out_1.rearrange("(p j) t -> p j t", j=PACK)
 
@@ -194,20 +194,20 @@ def tile_mix_lrbwd_none_kernel(tc, dy, w4_words, w4_scales, bu, ad, out_0, out_1
         quantize(dy_q[0], E5M2, 1)
         prepare_bu()
         h_chunk(0)
+        interleave("scalar", h_q[0], h_sb[0][:], HALF, W)
         for c in range(1, CHUNKS):
             prepare(dy_q[c], dy_raw[c][:], E5M2)
             h_chunk(c)
         open_group(0)
+        interleave("scalar", h_q[1], h_sb[1][:], HALF, W)
         interleave("vector", h_q[0], h_sb[0][:], 0, HALF)
-        interleave("vector", h_q[0], h_sb[0][:], HALF, W)
         ad_interleave(0)
         quantize(h_q[0], E5M2, 0)
         quantize(h_q[0], E5M2, 1)
         ad_quantize(0)
-        ad_interleave(1)
-        interleave("scalar", h_q[1], h_sb[1][:], HALF, W)
         close_group(0, 0, 2)
         open_group(1)
+        ad_interleave(1)
         interleave("vector", h_q[1], h_sb[1][:], 0, HALF)
         ad_quantize(1)
         close_group(0, 2, 4)
@@ -219,10 +219,6 @@ def tile_mix_lrbwd_none_kernel(tc, dy, w4_words, w4_scales, bu, ad, out_0, out_1
         ad_quantize(2)
         ad_quantize(3)
         prepare(h_q[2], h_sb[2][:], E5M2)
-        for n in (2, 3):
+        for n in range(2, len(groups)):
             open_group(n)
             close_group(n)
-        open_group(4)
-        open_group(5)
-        close_group(4)
-        close_group(5)

@@ -19,12 +19,13 @@ PACK = 4
 W = 512
 HALF = W // 2
 CHUNKS = T // W
-K_TILES = K // P
-BANKS = 8
-GROUP = W // P
+ALIGN = 256
 DY_VECTOR = 344
-SHARED_FROM = 3
-LAST_STORES = [2, 4]
+H0_VECTOR = 384
+H2_VECTOR = 344
+SHARED_FROM = 8
+H_LAST_AT = 16
+STORES = [(0, 5, 0, 1), (0, 5, 1, 1), (5, 3, 0, 2), (0, 4, 2, 1), (4, 4, 2, 1)]
 
 
 def tile_mix_lrbwd_none_kernel(tc, dy, w4_words, w4_scales, bu, ad, out_0, out_1):
@@ -34,10 +35,10 @@ def tile_mix_lrbwd_none_kernel(tc, dy, w4_words, w4_scales, bu, ad, out_0, out_1
         ps = ctx.enter_context(tc.psum_pool(name="ps", bufs=1))
         ctx.enter_context(tc.manual_schedule())
 
-        def operand(name):
-            grouped = sb.tile([P, W * PACK], BF16, name=name + "_bf", align_bytes=256)
-            codes = sb.tile([P, W], U32, name=name + "_codes", align_bytes=256)
-            scales = sb.tile([P, W], U8, name=name + "_scales", align_bytes=256)
+        def operand(name, width):
+            grouped = sb.tile([P, width * PACK], BF16, name=name + "_bf", align_bytes=ALIGN)
+            codes = sb.tile([P, width], U32, name=name + "_codes", align_bytes=ALIGN)
+            scales = sb.tile([P, width], U8, name=name + "_scales", align_bytes=ALIGN)
             return grouped, codes, scales
 
         def copy(engine, out, in_):
@@ -46,94 +47,93 @@ def tile_mix_lrbwd_none_kernel(tc, dy, w4_words, w4_scales, bu, ad, out_0, out_1
             else:
                 nc.scalar.copy(out=out, in_=in_)
 
-        def interleave(engine, op, raw, lo, hi, at=0):
-            src = raw[:, :, at + lo : at + hi].rearrange("p j (c i) -> p c j i", i=4)
+        def interleave(engine, op, raw, lo, hi):
+            src = raw[:, :, lo:hi].rearrange("p j (c i) -> p c j i", i=4)
             dst = op[0][:, lo * PACK : hi * PACK].rearrange("p (c i j) -> p c j i", i=4, j=PACK)
             copy(engine, dst, src)
 
-        def quantize(op, fmt, half):
+        def quantize(op, fmt, lo, hi):
             grouped, codes, scales = op
-            cols = slice(half * HALF, (half + 1) * HALF)
             nc.vector.quantize_mx(
-                out=codes[:, cols].bitcast(fmt),
-                scales=scales[:, cols],
-                in_=grouped[:, half * HALF * PACK : (half + 1) * HALF * PACK],
+                out=codes[:, lo:hi].bitcast(fmt),
+                scales=scales[:, lo:hi],
+                in_=grouped[:, lo * PACK : hi * PACK],
             )
 
-        def prepare(op, raw, fmt, at=0):
-            interleave("vector", op, raw, 0, HALF, at)
-            interleave("vector", op, raw, HALF, W, at)
-            quantize(op, fmt, 0)
-            quantize(op, fmt, 1)
+        def prepare(op, raw, fmt, lo=0):
+            interleave("vector", op, raw, lo, lo + HALF)
+            interleave("vector", op, raw, lo + HALF, lo + W)
+            quantize(op, fmt, lo, lo + HALF)
+            quantize(op, fmt, lo + HALF, lo + W)
 
-        banks_used = []
-
-        def bank():
-            i = len(banks_used) % BANKS
-            banks_used.append(i)
+        def bank(i):
             return ps.tile([P, W], F32, name="acc", tag="bank%d" % i)
 
         dy_v = dy.rearrange("(p j) t -> p j t", j=PACK)
-        dy_raw = [sb.tile([P, PACK, W], F32, name="dy_raw%d" % c, align_bytes=256) for c in range(CHUNKS)]
+        dy_raw = [sb.tile([P, PACK, W], F32, name="dy_raw%d" % c, align_bytes=ALIGN) for c in range(CHUNKS)]
         ad_v = ad.rearrange("(p j) k -> p j k", j=PACK)
-        ad_raw = [sb.tile([P, PACK, W], F32, name="ad_raw%d" % a, align_bytes=256) for a in range(K // W)]
-        bu_raw = sb.tile([P, PACK, R], F32, align_bytes=256)
-        w4_codes = sb.tile([P, 2 * K], U8, align_bytes=256)
-        w4_plane = sb.tile([P, K], U8, align_bytes=256)
+        ad_raw = [sb.tile([P, PACK, W], F32, name="ad_raw%d" % a, align_bytes=ALIGN) for a in range(K // W)]
+        bu_raw = sb.tile([P, PACK, R], F32, align_bytes=ALIGN)
+        w4_codes = sb.tile([P, 2 * K], U8, align_bytes=ALIGN)
+        w4_plane = sb.tile([P, K], U8, align_bytes=ALIGN)
 
         nc.gpsimd.memset(w4_plane[:].bitcast(I32), 0)
-        nc.sync.dma_start(out=dy_raw[0][:], in_=dy_v[:, :, 0:W])
-        nc.sync.dma_start(out=bu_raw[:], in_=bu.rearrange("(p j) r -> p j r", j=PACK))
         for q in range(4):
             nc.gpsimd.dma_start(
                 out=w4_plane[32 * q : 32 * q + 4, :].bitcast(I32),
                 in_=w4_scales[0, 4 * q : 4 * q + 4, :].bitcast(I32),
             )
-        for c in range(1, CHUNKS):
-            nc.sync.dma_start(out=dy_raw[c][:], in_=dy_v[:, :, c * W : (c + 1) * W])
+        nc.sync.dma_start(out=dy_raw[0][:, :, 0:HALF], in_=dy_v[:, :, 0:HALF])
+        nc.scalar.dma_start(out=dy_raw[0][:, :, HALF:W], in_=dy_v[:, :, HALF:W])
+        nc.sync.dma_start(out=bu_raw[:], in_=bu.rearrange("(p j) r -> p j r", j=PACK))
+        nc.sync.dma_start(out=dy_raw[1][:], in_=dy_v[:, :, W : 2 * W])
         nc.sync.dma_start(out=w4_codes[:].bitcast(I32), in_=w4_words[0].bitcast(I32))
-        for a in range(K // W):
-            nc.sync.dma_start(out=ad_raw[a][:], in_=ad_v[:, :, a * W : (a + 1) * W])
+        nc.sync.dma_start(out=ad_raw[0][:], in_=ad_v[:, :, 0:W])
+        nc.sync.dma_start(out=ad_raw[1][:], in_=ad_v[:, :, W:K])
+        nc.sync.dma_start(out=dy_raw[2][:], in_=dy_v[:, :, 2 * W : T])
 
-        dy_q = [operand("dy%d" % c) for c in range(CHUNKS)]
-        h_q = [operand("h%d" % c) for c in range(CHUNKS)]
-        ad_q = [operand("ad%d" % a) for a in range(K // W)]
-        bu_q = operand("bu")
-        h_sb = [sb.tile([P, PACK, W], F32, name="h_sb%d" % c, align_bytes=256) for c in range(CHUNKS)]
-        groups = [(0, 4, 0, 1), (0, 4, 1, 1), (4, 2, 0, 2), (6, 2, 0, 2), (0, 4, 2, 1), (4, 4, 2, 1)]
-        dx_sb = [sb.tile([P, nk, nch * W], F32, name="dx_sb%d" % n, align_bytes=256) for n, (k0, nk, c0, nch) in enumerate(groups)]
+        dy_q = [operand("dy%d" % c, W) for c in range(CHUNKS)]
+        h_q = [operand("h%d" % c, W) for c in range(CHUNKS)]
+        ad_q = [operand("ad%d" % a, W) for a in range(K // W)]
+        bu_q = operand("bu", R)
+        h_first = sb.tile([P, PACK, 2 * W], F32, align_bytes=ALIGN)
+        h_last = sb.tile([P, PACK, W], F32, align_bytes=ALIGN)
+        h_sb = [h_first[:, :, 0:W], h_first[:, :, W : 2 * W], h_last[:]]
+        dx_sb = [
+            sb.tile([P, nk, nch * W], F32, name="dx_sb%d" % n, align_bytes=ALIGN)
+            for n, (k0, nk, c0, nch) in enumerate(STORES)
+        ]
         dx_out = out_0.rearrange("(g p) t -> p g t", p=P)
         h_out = out_1.rearrange("(p j) t -> p j t", j=PACK)
 
-        def prepare_bu():
-            dst = bu_q[0][:].rearrange("p (s m j) -> p m j s", s=PACK, j=PACK)
-            src = bu_raw[:].rearrange("p j (m s) -> p m j s", s=PACK)
-            nc.vector.tensor_copy(out=dst[:, 0:80], in_=src[:, 0:80])
-            nc.scalar.copy(out=dst[:, 80:128], in_=src[:, 80:128])
-            quantize(bu_q, E4M3, 0)
-            quantize(bu_q, E4M3, 1)
+        def bu_interleave(engine, s):
+            dst = bu_q[0][:].rearrange("p (s m j) -> p s m j", s=PACK, j=PACK)
+            src = bu_raw[:].rearrange("p j (m s) -> p s m j", s=PACK)
+            copy(engine, dst[:, s], src[:, s])
 
-        def h_chunk(c):
-            for j in range(PACK):
-                acc = bank()
-                cols = slice(j * P, (j + 1) * P)
-                nc.tensor.matmul_mx(
-                    out=acc[:],
-                    lhsT=bu_q[1][:, cols].bitcast(E4M3),
-                    lhsT_scale=bu_q[2][:, cols],
-                    rhs=dy_q[c][1][:].bitcast(E5M2),
-                    rhs_scale=dy_q[c][2][:],
-                    start=True,
-                    stop=True,
-                )
-                nc.scalar.copy(out=h_sb[c][:, j, :], in_=acc[:])
-            nc.sync.dma_start(out=h_out[:, :, c * W : (c + 1) * W], in_=h_sb[c][:])
+        def h_pass(c, j, b, engine):
+            acc = bank(b)
+            cols = slice(j * P, (j + 1) * P)
+            nc.tensor.matmul_mx(
+                out=acc[:],
+                lhsT=bu_q[1][:, cols].bitcast(E4M3),
+                lhsT_scale=bu_q[2][:, cols],
+                rhs=dy_q[c][1][:].bitcast(E5M2),
+                rhs_scale=dy_q[c][2][:],
+                start=True,
+                stop=True,
+            )
+            copy(engine, h_sb[c][:, j, :], acc[:])
 
+        tiles = [
+            (n, k, c) for n, (k0, nk, c0, nch) in enumerate(STORES) for c in range(c0, c0 + nch) for k in range(k0, k0 + nk)
+        ]
         open_banks = {}
 
-        def base_pass(k, c):
-            acc = bank()
-            open_banks[k, c] = acc
+        def base_pass(i):
+            n, k, c = tiles[i]
+            acc = bank((i + 4 + (PACK if i >= H_LAST_AT else 0)) % 8)
+            open_banks[i] = acc
             nc.tensor.matmul_mx(
                 out=acc[:],
                 lhsT=w4_codes[:, 2 * k * P : 2 * (k + 1) * P].bitcast(E2M1),
@@ -144,11 +144,13 @@ def tile_mix_lrbwd_none_kernel(tc, dy, w4_words, w4_scales, bu, ad, out_0, out_1
                 stop=False,
             )
 
-        def adapter_pass(k, c):
-            a, g = divmod(k, GROUP)
+        def adapter_pass(i):
+            n, k, c = tiles[i]
+            k0, nk, c0, nch = STORES[n]
+            a, g = divmod(k, W // P)
             cols = slice(g * P, (g + 1) * P)
             nc.tensor.matmul_mx(
-                out=open_banks[k, c][:],
+                out=open_banks[i][:],
                 lhsT=ad_q[a][1][:, cols].bitcast(E4M3),
                 lhsT_scale=ad_q[a][2][:, cols],
                 rhs=h_q[c][1][:].bitcast(E5M2),
@@ -156,69 +158,72 @@ def tile_mix_lrbwd_none_kernel(tc, dy, w4_words, w4_scales, bu, ad, out_0, out_1
                 start=False,
                 stop=True,
             )
+            engine = "vector" if i >= SHARED_FROM and i % 2 == 1 else "scalar"
+            copy(engine, dx_sb[n][:, k - k0, (c - c0) * W : (c - c0 + 1) * W], open_banks[i][:])
+            if i + 1 == len(tiles) or tiles[i + 1][0] != n:
+                nc.sync.dma_start(out=dx_out[:, k0 : k0 + nk, c0 * W : (c0 + nch) * W], in_=dx_sb[n][:])
 
-        def ad_interleave(n):
-            a, half = divmod(n, 2)
-            interleave("vector", ad_q[a], ad_raw[a][:], half * HALF, (half + 1) * HALF)
-
-        def ad_quantize(n):
-            a, half = divmod(n, 2)
-            quantize(ad_q[a], E4M3, half)
-
-        def members(n):
-            k0, nk, c0, nch = groups[n]
-            return [(k, c) for k in range(k0, k0 + nk) for c in range(c0, c0 + nch)]
-
-        def open_group(n):
-            for k, c in members(n):
-                base_pass(k, c)
-
-        def close_group(n, first=0, last=GROUP):
-            k0, nk, c0, nch = groups[n]
-            ends = LAST_STORES if n == len(groups) - 1 else [GROUP]
+        def open_tiles(first, last):
             for i in range(first, last):
-                k, c = members(n)[i]
-                adapter_pass(k, c)
-                engine = "vector" if n >= SHARED_FROM and i % 2 == 0 else "scalar"
-                copy(engine, dx_sb[n][:, k - k0, (c - c0) * W : (c - c0 + 1) * W], open_banks[k, c][:])
-                if i + 1 in ends:
-                    g0 = ([0] + ends)[ends.index(i + 1)] // nch
-                    nc.sync.dma_start(
-                        out=dx_out[:, k0 + g0 : k + 1, c0 * W : (c0 + nch) * W], in_=dx_sb[n][:, g0 : k + 1 - k0, :]
-                    )
+                base_pass(i)
+
+        def close_tiles(first, last):
+            for i in range(first, last):
+                adapter_pass(i)
 
         interleave("vector", dy_q[0], dy_raw[0][:], 0, HALF)
         interleave("vector", dy_q[0], dy_raw[0][:], HALF, DY_VECTOR)
         interleave("scalar", dy_q[0], dy_raw[0][:], DY_VECTOR, W)
-        quantize(dy_q[0], E5M2, 0)
-        quantize(dy_q[0], E5M2, 1)
-        prepare_bu()
-        h_chunk(0)
-        interleave("scalar", h_q[0], h_sb[0][:], HALF, W)
-        for c in range(1, CHUNKS):
-            prepare(dy_q[c], dy_raw[c][:], E5M2)
-            h_chunk(c)
-        open_group(0)
-        interleave("scalar", h_q[1], h_sb[1][:], HALF, W)
-        interleave("vector", h_q[0], h_sb[0][:], 0, HALF)
-        ad_interleave(0)
-        quantize(h_q[0], E5M2, 0)
-        quantize(h_q[0], E5M2, 1)
-        ad_quantize(0)
-        close_group(0, 0, 2)
-        open_group(1)
-        ad_interleave(1)
-        interleave("vector", h_q[1], h_sb[1][:], 0, HALF)
-        ad_quantize(1)
-        close_group(0, 2, 4)
-        quantize(h_q[1], E5M2, 0)
-        quantize(h_q[1], E5M2, 1)
-        close_group(1)
-        ad_interleave(2)
-        ad_interleave(3)
-        ad_quantize(2)
-        ad_quantize(3)
-        prepare(h_q[2], h_sb[2][:], E5M2)
-        for n in range(2, len(groups)):
-            open_group(n)
-            close_group(n)
+        quantize(dy_q[0], E5M2, 0, HALF)
+        quantize(dy_q[0], E5M2, HALF, W)
+        bu_interleave("vector", 0)
+        bu_interleave("scalar", 1)
+        bu_interleave("vector", 2)
+        bu_interleave("scalar", 3)
+        for j in range(PACK):
+            quantize(bu_q, E4M3, j * P, (j + 1) * P)
+            h_pass(0, j, j, "scalar")
+        open_tiles(0, 4)
+        interleave("scalar", h_q[0], h_sb[0], H0_VECTOR, W)
+        prepare(dy_q[1], dy_raw[1][:], E5M2)
+        interleave("vector", h_q[0], h_sb[0], 0, H0_VECTOR)
+        interleave("vector", ad_q[0], ad_raw[0][:], 0, HALF)
+        for b in range(PACK):
+            h_pass(1, (b + PACK - 1) % PACK, b, "vector" if b == PACK - 1 else "scalar")
+        nc.sync.dma_start(out=h_out[:, :, 0 : 2 * W], in_=h_first[:])
+        open_tiles(4, 8)
+        interleave("scalar", ad_q[0], ad_raw[0][:], HALF, W)
+        quantize(h_q[0], E5M2, 0, W)
+        quantize(ad_q[0], E4M3, 0, HALF)
+        close_tiles(0, 2)
+        interleave("vector", h_q[1], h_sb[1], 0, HALF)
+        quantize(ad_q[0], E4M3, HALF, W)
+        close_tiles(2, 4)
+        open_tiles(8, 10)
+        interleave("vector", ad_q[1], ad_raw[1][:], 0, P)
+        interleave("vector", h_q[1], h_sb[1], HALF, W)
+        quantize(ad_q[1], E4M3, 0, P)
+        close_tiles(4, 5)
+        open_tiles(10, 12)
+        quantize(h_q[1], E5M2, 0, W)
+        interleave("vector", ad_q[1], ad_raw[1][:], P, W)
+        interleave("vector", dy_q[2], dy_raw[2][:], 0, HALF)
+        quantize(ad_q[1], E4M3, P, HALF)
+        quantize(ad_q[1], E4M3, HALF, W)
+        interleave("vector", dy_q[2], dy_raw[2][:], HALF, W)
+        close_tiles(5, 8)
+        open_tiles(12, 14)
+        close_tiles(8, 10)
+        quantize(dy_q[2], E5M2, 0, W)
+        open_tiles(14, 16)
+        close_tiles(10, 16)
+        for j in range(PACK):
+            h_pass(2, j, 4 + j, "vector" if j % 2 else "scalar")
+        nc.sync.dma_start(out=h_out[:, :, 2 * W : T], in_=h_last[:])
+        open_tiles(16, 24)
+        interleave("vector", h_q[2], h_sb[2], 0, HALF)
+        interleave("scalar", h_q[2], h_sb[2], H2_VECTOR, W)
+        interleave("vector", h_q[2], h_sb[2], HALF, H2_VECTOR)
+        quantize(h_q[2], E5M2, 0, HALF)
+        quantize(h_q[2], E5M2, HALF, W)
+        close_tiles(16, 24)

@@ -21,7 +21,9 @@ HALF = W // 2
 CHUNKS = T // W
 ALIGN = 256
 DY_VECTOR = 344
+BU_VECTOR = 80
 H0_VECTOR = 384
+H1_VECTOR = 384
 H2_VECTOR = 344
 SHARED_FROM = 8
 H_LAST_AT = 16
@@ -83,8 +85,7 @@ def tile_mix_lrbwd_none_kernel(tc, dy, w4_words, w4_scales, bu, ad, out_0, out_1
                 out=w4_plane[32 * q : 32 * q + 4, :].bitcast(I32),
                 in_=w4_scales[0, 4 * q : 4 * q + 4, :].bitcast(I32),
             )
-        nc.sync.dma_start(out=dy_raw[0][:, :, 0:HALF], in_=dy_v[:, :, 0:HALF])
-        nc.scalar.dma_start(out=dy_raw[0][:, :, HALF:W], in_=dy_v[:, :, HALF:W])
+        nc.sync.dma_start(out=dy_raw[0][:], in_=dy_v[:, :, 0:W])
         nc.sync.dma_start(out=bu_raw[:], in_=bu.rearrange("(p j) r -> p j r", j=PACK))
         nc.sync.dma_start(out=dy_raw[1][:], in_=dy_v[:, :, W : 2 * W])
         nc.sync.dma_start(out=w4_codes[:].bitcast(I32), in_=w4_words[0].bitcast(I32))
@@ -96,9 +97,7 @@ def tile_mix_lrbwd_none_kernel(tc, dy, w4_words, w4_scales, bu, ad, out_0, out_1
         h_q = [operand("h%d" % c, W) for c in range(CHUNKS)]
         ad_q = [operand("ad%d" % a, W) for a in range(K // W)]
         bu_q = operand("bu", R)
-        h_first = sb.tile([P, PACK, 2 * W], F32, align_bytes=ALIGN)
-        h_last = sb.tile([P, PACK, W], F32, align_bytes=ALIGN)
-        h_sb = [h_first[:, :, 0:W], h_first[:, :, W : 2 * W], h_last[:]]
+        h_sb = [sb.tile([P, PACK, W], F32, name="h_sb%d" % c, align_bytes=ALIGN) for c in range(CHUNKS)]
         dx_sb = [
             sb.tile([P, nk, nch * W], F32, name="dx_sb%d" % n, align_bytes=ALIGN)
             for n, (k0, nk, c0, nch) in enumerate(STORES)
@@ -106,10 +105,10 @@ def tile_mix_lrbwd_none_kernel(tc, dy, w4_words, w4_scales, bu, ad, out_0, out_1
         dx_out = out_0.rearrange("(g p) t -> p g t", p=P)
         h_out = out_1.rearrange("(p j) t -> p j t", j=PACK)
 
-        def bu_interleave(engine, s):
-            dst = bu_q[0][:].rearrange("p (s m j) -> p s m j", s=PACK, j=PACK)
-            src = bu_raw[:].rearrange("p j (m s) -> p s m j", s=PACK)
-            copy(engine, dst[:, s], src[:, s])
+        def bu_interleave(engine, lo, hi):
+            dst = bu_q[0][:].rearrange("p (s m j) -> p m j s", s=PACK, j=PACK)
+            src = bu_raw[:].rearrange("p j (m s) -> p m j s", s=PACK)
+            copy(engine, dst[:, lo:hi], src[:, lo:hi])
 
         def h_pass(c, j, b, engine):
             acc = bank(b)
@@ -124,6 +123,11 @@ def tile_mix_lrbwd_none_kernel(tc, dy, w4_words, w4_scales, bu, ad, out_0, out_1
                 stop=True,
             )
             copy(engine, h_sb[c][:, j, :], acc[:])
+
+        def h_chunk(c, first_bank, engines):
+            for j in range(PACK):
+                h_pass(c, j, first_bank + j, engines[j % len(engines)])
+            nc.sync.dma_start(out=h_out[:, :, c * W : (c + 1) * W], in_=h_sb[c][:])
 
         tiles = [
             (n, k, c) for n, (k0, nk, c0, nch) in enumerate(STORES) for c in range(c0, c0 + nch) for k in range(k0, k0 + nk)
@@ -176,39 +180,36 @@ def tile_mix_lrbwd_none_kernel(tc, dy, w4_words, w4_scales, bu, ad, out_0, out_1
         interleave("scalar", dy_q[0], dy_raw[0][:], DY_VECTOR, W)
         quantize(dy_q[0], E5M2, 0, HALF)
         quantize(dy_q[0], E5M2, HALF, W)
-        bu_interleave("vector", 0)
-        bu_interleave("scalar", 1)
-        bu_interleave("vector", 2)
-        bu_interleave("scalar", 3)
-        for j in range(PACK):
-            quantize(bu_q, E4M3, j * P, (j + 1) * P)
-            h_pass(0, j, j, "scalar")
-        open_tiles(0, 4)
-        interleave("scalar", h_q[0], h_sb[0], H0_VECTOR, W)
+        bu_interleave("vector", 0, BU_VECTOR)
+        bu_interleave("scalar", BU_VECTOR, P)
+        quantize(bu_q, E4M3, 0, HALF)
+        quantize(bu_q, E4M3, HALF, W)
+        h_chunk(0, 0, ["scalar"])
+        interleave("scalar", h_q[0], h_sb[0][:], H0_VECTOR, W)
         prepare(dy_q[1], dy_raw[1][:], E5M2)
-        interleave("vector", h_q[0], h_sb[0], 0, H0_VECTOR)
+        h_chunk(1, 0, ["scalar"])
+        open_tiles(0, 7)
+        interleave("scalar", h_q[1], h_sb[1][:], H1_VECTOR, W)
+        interleave("vector", h_q[0], h_sb[0][:], 0, H0_VECTOR)
         interleave("vector", ad_q[0], ad_raw[0][:], 0, HALF)
-        for b in range(PACK):
-            h_pass(1, (b + PACK - 1) % PACK, b, "vector" if b == PACK - 1 else "scalar")
-        nc.sync.dma_start(out=h_out[:, :, 0 : 2 * W], in_=h_first[:])
-        open_tiles(4, 8)
-        interleave("scalar", ad_q[0], ad_raw[0][:], HALF, W)
         quantize(h_q[0], E5M2, 0, W)
         quantize(ad_q[0], E4M3, 0, HALF)
         close_tiles(0, 2)
-        interleave("vector", h_q[1], h_sb[1], 0, HALF)
+        open_tiles(7, 8)
+        interleave("vector", ad_q[0], ad_raw[0][:], HALF, W)
+        interleave("vector", ad_q[1], ad_raw[1][:], 0, P)
         quantize(ad_q[0], E4M3, HALF, W)
+        quantize(ad_q[1], E4M3, 0, P)
         close_tiles(2, 4)
         open_tiles(8, 10)
-        interleave("vector", ad_q[1], ad_raw[1][:], 0, P)
-        interleave("vector", h_q[1], h_sb[1], HALF, W)
-        quantize(ad_q[1], E4M3, 0, P)
         close_tiles(4, 5)
         open_tiles(10, 12)
+        interleave("vector", h_q[1], h_sb[1][:], 0, H1_VECTOR)
+        interleave("vector", ad_q[1], ad_raw[1][:], P, HALF)
         quantize(h_q[1], E5M2, 0, W)
-        interleave("vector", ad_q[1], ad_raw[1][:], P, W)
-        interleave("vector", dy_q[2], dy_raw[2][:], 0, HALF)
+        interleave("vector", ad_q[1], ad_raw[1][:], HALF, W)
         quantize(ad_q[1], E4M3, P, HALF)
+        interleave("vector", dy_q[2], dy_raw[2][:], 0, HALF)
         quantize(ad_q[1], E4M3, HALF, W)
         interleave("vector", dy_q[2], dy_raw[2][:], HALF, W)
         close_tiles(5, 8)
@@ -217,13 +218,11 @@ def tile_mix_lrbwd_none_kernel(tc, dy, w4_words, w4_scales, bu, ad, out_0, out_1
         quantize(dy_q[2], E5M2, 0, W)
         open_tiles(14, 16)
         close_tiles(10, 16)
-        for j in range(PACK):
-            h_pass(2, j, 4 + j, "vector" if j % 2 else "scalar")
-        nc.sync.dma_start(out=h_out[:, :, 2 * W : T], in_=h_last[:])
+        h_chunk(2, 4, ["scalar", "vector"])
         open_tiles(16, 24)
-        interleave("vector", h_q[2], h_sb[2], 0, HALF)
-        interleave("scalar", h_q[2], h_sb[2], H2_VECTOR, W)
-        interleave("vector", h_q[2], h_sb[2], HALF, H2_VECTOR)
+        interleave("vector", h_q[2], h_sb[2][:], 0, HALF)
+        interleave("scalar", h_q[2], h_sb[2][:], H2_VECTOR, W)
+        interleave("vector", h_q[2], h_sb[2][:], HALF, H2_VECTOR)
         quantize(h_q[2], E5M2, 0, HALF)
         quantize(h_q[2], E5M2, HALF, W)
         close_tiles(16, 24)

@@ -23,11 +23,10 @@ ALIGN = 256
 DY_VECTOR = 344
 BU_VECTOR = 80
 H0_VECTOR = 384
-H1_VECTOR = 384
-H2_VECTOR = 344
-SHARED_FROM = 8
-H_LAST_AT = 16
-STORES = [(0, 5, 0, 1), (0, 5, 1, 1), (5, 3, 0, 2), (0, 4, 2, 1), (4, 4, 2, 1)]
+H1_VECTOR = 336
+SHARED_ONCE = 7
+SHARED_FROM = 16
+STORES = [(0, 4, 0, 1), (0, 4, 1, 1), (4, 4, 0, 1), (4, 4, 1, 1), (0, 4, 2, 1), (4, 4, 2, 1)]
 
 
 def tile_mix_lrbwd_none_kernel(tc, dy, w4_words, w4_scales, bu, ad, out_0, out_1):
@@ -88,8 +87,8 @@ def tile_mix_lrbwd_none_kernel(tc, dy, w4_words, w4_scales, bu, ad, out_0, out_1
         nc.sync.dma_start(out=dy_raw[0][:], in_=dy_v[:, :, 0:W])
         nc.sync.dma_start(out=bu_raw[:], in_=bu.rearrange("(p j) r -> p j r", j=PACK))
         nc.sync.dma_start(out=dy_raw[1][:], in_=dy_v[:, :, W : 2 * W])
-        nc.sync.dma_start(out=w4_codes[:].bitcast(I32), in_=w4_words[0].bitcast(I32))
         nc.sync.dma_start(out=ad_raw[0][:], in_=ad_v[:, :, 0:W])
+        nc.sync.dma_start(out=w4_codes[:].bitcast(I32), in_=w4_words[0].bitcast(I32))
         nc.sync.dma_start(out=ad_raw[1][:], in_=ad_v[:, :, W:K])
         nc.sync.dma_start(out=dy_raw[2][:], in_=dy_v[:, :, 2 * W : T])
 
@@ -136,7 +135,7 @@ def tile_mix_lrbwd_none_kernel(tc, dy, w4_words, w4_scales, bu, ad, out_0, out_1
 
         def base_pass(i):
             n, k, c = tiles[i]
-            acc = bank((i + 4 + (PACK if i >= H_LAST_AT else 0)) % 8)
+            acc = bank((i + 4) % 8)
             open_banks[i] = acc
             nc.tensor.matmul_mx(
                 out=acc[:],
@@ -162,7 +161,7 @@ def tile_mix_lrbwd_none_kernel(tc, dy, w4_words, w4_scales, bu, ad, out_0, out_1
                 start=False,
                 stop=True,
             )
-            engine = "vector" if i >= SHARED_FROM and i % 2 == 1 else "scalar"
+            engine = "vector" if i == SHARED_ONCE or (i >= SHARED_FROM and i % 2 == 1) else "scalar"
             copy(engine, dx_sb[n][:, k - k0, (c - c0) * W : (c - c0 + 1) * W], open_banks[i][:])
             if i + 1 == len(tiles) or tiles[i + 1][0] != n:
                 nc.sync.dma_start(out=dx_out[:, k0 : k0 + nk, c0 * W : (c0 + nch) * W], in_=dx_sb[n][:])
@@ -188,41 +187,35 @@ def tile_mix_lrbwd_none_kernel(tc, dy, w4_words, w4_scales, bu, ad, out_0, out_1
         interleave("scalar", h_q[0], h_sb[0][:], H0_VECTOR, W)
         prepare(dy_q[1], dy_raw[1][:], E5M2)
         h_chunk(1, 0, ["scalar"])
-        open_tiles(0, 7)
+        open_tiles(0, 6)
         interleave("scalar", h_q[1], h_sb[1][:], H1_VECTOR, W)
-        interleave("vector", h_q[0], h_sb[0][:], 0, H0_VECTOR)
         interleave("vector", ad_q[0], ad_raw[0][:], 0, HALF)
-        quantize(h_q[0], E5M2, 0, W)
+        interleave("vector", h_q[0], h_sb[0][:], 0, H0_VECTOR)
         quantize(ad_q[0], E4M3, 0, HALF)
+        quantize(h_q[0], E5M2, 0, W)
         close_tiles(0, 2)
-        open_tiles(7, 8)
+        open_tiles(6, 8)
         interleave("vector", ad_q[0], ad_raw[0][:], HALF, W)
-        interleave("vector", ad_q[1], ad_raw[1][:], 0, P)
+        interleave("vector", h_q[1], h_sb[1][:], 0, P)
         quantize(ad_q[0], E4M3, HALF, W)
-        quantize(ad_q[1], E4M3, 0, P)
         close_tiles(2, 4)
         open_tiles(8, 10)
-        close_tiles(4, 5)
-        open_tiles(10, 12)
-        interleave("vector", h_q[1], h_sb[1][:], 0, H1_VECTOR)
-        interleave("vector", ad_q[1], ad_raw[1][:], P, HALF)
+        interleave("vector", h_q[1], h_sb[1][:], P, H1_VECTOR)
+        interleave("vector", ad_q[1], ad_raw[1][:], 0, P)
         quantize(h_q[1], E5M2, 0, W)
+        interleave("vector", ad_q[1], ad_raw[1][:], P, HALF)
         interleave("vector", ad_q[1], ad_raw[1][:], HALF, W)
-        quantize(ad_q[1], E4M3, P, HALF)
-        interleave("vector", dy_q[2], dy_raw[2][:], 0, HALF)
+        quantize(ad_q[1], E4M3, 0, HALF)
         quantize(ad_q[1], E4M3, HALF, W)
-        interleave("vector", dy_q[2], dy_raw[2][:], HALF, W)
-        close_tiles(5, 8)
-        open_tiles(12, 14)
-        close_tiles(8, 10)
-        quantize(dy_q[2], E5M2, 0, W)
-        open_tiles(14, 16)
-        close_tiles(10, 16)
+        close_tiles(4, 8)
+        open_tiles(10, 12)
+        prepare(dy_q[2], dy_raw[2][:], E5M2)
+        close_tiles(8, 12)
+        open_tiles(12, 16)
         h_chunk(2, 4, ["scalar", "vector"])
-        open_tiles(16, 24)
-        interleave("vector", h_q[2], h_sb[2][:], 0, HALF)
-        interleave("scalar", h_q[2], h_sb[2][:], H2_VECTOR, W)
-        interleave("vector", h_q[2], h_sb[2][:], HALF, H2_VECTOR)
-        quantize(h_q[2], E5M2, 0, HALF)
-        quantize(h_q[2], E5M2, HALF, W)
-        close_tiles(16, 24)
+        prepare(h_q[2], h_sb[2][:], E5M2)
+        close_tiles(12, 16)
+        open_tiles(16, 22)
+        close_tiles(16, 20)
+        open_tiles(22, 24)
+        close_tiles(20, 24)

@@ -84,8 +84,8 @@ def tile_mix_lrbwd_none_kernel(tc, dy, w4_words, w4_scales, bu, ad, out_0, out_1
                 out=w4_plane[32 * q : 32 * q + 4, :].bitcast(I32),
                 in_=w4_scales[0, 4 * q : 4 * q + 4, :].bitcast(I32),
             )
-        nc.sync.dma_start(out=dy_raw[0][:], in_=dy_v[:, :, 0:W])
         nc.sync.dma_start(out=bu_raw[:], in_=bu.rearrange("(p j) r -> p j r", j=PACK))
+        nc.sync.dma_start(out=dy_raw[0][:], in_=dy_v[:, :, 0:W])
         nc.sync.dma_start(out=dy_raw[1][:], in_=dy_v[:, :, W : 2 * W])
         nc.sync.dma_start(out=ad_raw[0][:], in_=ad_v[:, :, 0:W])
         nc.sync.dma_start(out=w4_codes[:].bitcast(I32), in_=w4_words[0].bitcast(I32))
@@ -174,15 +174,15 @@ def tile_mix_lrbwd_none_kernel(tc, dy, w4_words, w4_scales, bu, ad, out_0, out_1
             for i in range(first, last):
                 adapter_pass(i)
 
+        bu_interleave("vector", 0, BU_VECTOR)
+        bu_interleave("scalar", BU_VECTOR, P)
+        quantize(bu_q, E4M3, 0, HALF)
+        quantize(bu_q, E4M3, HALF, W)
         interleave("vector", dy_q[0], dy_raw[0][:], 0, HALF)
         interleave("vector", dy_q[0], dy_raw[0][:], HALF, DY_VECTOR)
         interleave("scalar", dy_q[0], dy_raw[0][:], DY_VECTOR, W)
         quantize(dy_q[0], E5M2, 0, HALF)
         quantize(dy_q[0], E5M2, HALF, W)
-        bu_interleave("vector", 0, BU_VECTOR)
-        bu_interleave("scalar", BU_VECTOR, P)
-        quantize(bu_q, E4M3, 0, HALF)
-        quantize(bu_q, E4M3, HALF, W)
         h_chunk(0, 0, ["scalar"])
         interleave("scalar", h_q[0], h_sb[0][:], H0_VECTOR, W)
         prepare(dy_q[1], dy_raw[1][:], E5M2)

@@ -19,14 +19,11 @@ PACK = 4
 W = 512
 HALF = W // 2
 CHUNKS = T // W
+K_TILES = K // P
+BANKS = 8
 ALIGN = 256
-DY_VECTOR = 344
 BU_VECTOR = 80
-H0_VECTOR = 384
-H1_VECTOR = 336
-SHARED_ONCE = 7
-SHARED_FROM = 16
-STORES = [(0, 4, 0, 1), (0, 4, 1, 1), (4, 4, 0, 1), (4, 4, 1, 1), (0, 4, 2, 1), (4, 4, 2, 1)]
+H2_SCALAR = 352
 
 
 def tile_mix_lrbwd_none_kernel(tc, dy, w4_words, w4_scales, bu, ad, out_0, out_1):
@@ -61,19 +58,18 @@ def tile_mix_lrbwd_none_kernel(tc, dy, w4_words, w4_scales, bu, ad, out_0, out_1
                 in_=grouped[:, lo * PACK : hi * PACK],
             )
 
-        def prepare(op, raw, fmt, lo=0):
-            interleave("vector", op, raw, lo, lo + HALF)
-            interleave("vector", op, raw, lo + HALF, lo + W)
-            quantize(op, fmt, lo, lo + HALF)
-            quantize(op, fmt, lo + HALF, lo + W)
+        def prepare(op, raw, fmt):
+            interleave("vector", op, raw, 0, HALF)
+            interleave("vector", op, raw, HALF, W)
+            quantize(op, fmt, 0, HALF)
+            quantize(op, fmt, HALF, W)
 
         def bank(i):
-            return ps.tile([P, W], F32, name="acc", tag="bank%d" % i)
+            return ps.tile([P, W], F32, name="acc", tag="bank%d" % (i % BANKS))
 
         dy_v = dy.rearrange("(p j) t -> p j t", j=PACK)
         dy_raw = [sb.tile([P, PACK, W], F32, name="dy_raw%d" % c, align_bytes=ALIGN) for c in range(CHUNKS)]
-        ad_v = ad.rearrange("(p j) k -> p j k", j=PACK)
-        ad_raw = [sb.tile([P, PACK, W], F32, name="ad_raw%d" % a, align_bytes=ALIGN) for a in range(K // W)]
+        ad_raw = sb.tile([P, PACK, K], F32, align_bytes=ALIGN)
         bu_raw = sb.tile([P, PACK, R], F32, align_bytes=ALIGN)
         w4_codes = sb.tile([P, 2 * K], U8, align_bytes=ALIGN)
         w4_plane = sb.tile([P, K], U8, align_bytes=ALIGN)
@@ -84,24 +80,21 @@ def tile_mix_lrbwd_none_kernel(tc, dy, w4_words, w4_scales, bu, ad, out_0, out_1
                 out=w4_plane[32 * q : 32 * q + 4, :].bitcast(I32),
                 in_=w4_scales[0, 4 * q : 4 * q + 4, :].bitcast(I32),
             )
-        nc.sync.dma_start(out=bu_raw[:], in_=bu.rearrange("(p j) r -> p j r", j=PACK))
         nc.sync.dma_start(out=dy_raw[0][:], in_=dy_v[:, :, 0:W])
-        nc.sync.dma_start(out=dy_raw[1][:], in_=dy_v[:, :, W : 2 * W])
-        nc.sync.dma_start(out=ad_raw[0][:], in_=ad_v[:, :, 0:W])
+        nc.sync.dma_start(out=bu_raw[:], in_=bu.rearrange("(p j) r -> p j r", j=PACK))
+        for c in range(1, CHUNKS):
+            nc.sync.dma_start(out=dy_raw[c][:], in_=dy_v[:, :, c * W : (c + 1) * W])
         nc.sync.dma_start(out=w4_codes[:].bitcast(I32), in_=w4_words[0].bitcast(I32))
-        nc.sync.dma_start(out=ad_raw[1][:], in_=ad_v[:, :, W:K])
-        nc.sync.dma_start(out=dy_raw[2][:], in_=dy_v[:, :, 2 * W : T])
+        nc.sync.dma_start(out=ad_raw[:], in_=ad.rearrange("(p j) k -> p j k", j=PACK))
 
         dy_q = [operand("dy%d" % c, W) for c in range(CHUNKS)]
         h_q = [operand("h%d" % c, W) for c in range(CHUNKS)]
-        ad_q = [operand("ad%d" % a, W) for a in range(K // W)]
+        ad_q = [operand("ad%d" % a, HALF) for a in range(K // HALF)]
         bu_q = operand("bu", R)
-        h_sb = [sb.tile([P, PACK, W], F32, name="h_sb%d" % c, align_bytes=ALIGN) for c in range(CHUNKS)]
-        dx_sb = [
-            sb.tile([P, nk, nch * W], F32, name="dx_sb%d" % n, align_bytes=ALIGN)
-            for n, (k0, nk, c0, nch) in enumerate(STORES)
-        ]
-        dx_out = out_0.rearrange("(g p) t -> p g t", p=P)
+        h_first = sb.tile([P, PACK, 2 * W], F32, align_bytes=ALIGN)
+        h_last = sb.tile([P, PACK, W], F32, align_bytes=ALIGN)
+        h_sb = [h_first[:, :, 0:W], h_first[:, :, W : 2 * W], h_last[:]]
+        dx_sb = [sb.tile([P, T], F32, name="dx_sb%d" % k, align_bytes=ALIGN) for k in range(K_TILES)]
         h_out = out_1.rearrange("(p j) t -> p j t", j=PACK)
 
         def bu_interleave(engine, lo, hi):
@@ -109,33 +102,30 @@ def tile_mix_lrbwd_none_kernel(tc, dy, w4_words, w4_scales, bu, ad, out_0, out_1
             src = bu_raw[:].rearrange("p j (m s) -> p m j s", s=PACK)
             copy(engine, dst[:, lo:hi], src[:, lo:hi])
 
-        def h_pass(c, j, b, engine):
-            acc = bank(b)
-            cols = slice(j * P, (j + 1) * P)
-            nc.tensor.matmul_mx(
-                out=acc[:],
-                lhsT=bu_q[1][:, cols].bitcast(E4M3),
-                lhsT_scale=bu_q[2][:, cols],
-                rhs=dy_q[c][1][:].bitcast(E5M2),
-                rhs_scale=dy_q[c][2][:],
-                start=True,
-                stop=True,
-            )
-            copy(engine, h_sb[c][:, j, :], acc[:])
+        def ad_interleave(a):
+            interleave("vector", ad_q[a], ad_raw[:, :, a * HALF : (a + 1) * HALF], 0, HALF)
 
-        def h_chunk(c, first_bank, engines):
+        def h_chunk(c, first_bank):
             for j in range(PACK):
-                h_pass(c, j, first_bank + j, engines[j % len(engines)])
-            nc.sync.dma_start(out=h_out[:, :, c * W : (c + 1) * W], in_=h_sb[c][:])
+                acc = bank(first_bank + j)
+                cols = slice(j * P, (j + 1) * P)
+                nc.tensor.matmul_mx(
+                    out=acc[:],
+                    lhsT=bu_q[1][:, cols].bitcast(E4M3),
+                    lhsT_scale=bu_q[2][:, cols],
+                    rhs=dy_q[c][1][:].bitcast(E5M2),
+                    rhs_scale=dy_q[c][2][:],
+                    start=True,
+                    stop=True,
+                )
+                copy("scalar", h_sb[c][:, j, :], acc[:])
 
-        tiles = [
-            (n, k, c) for n, (k0, nk, c0, nch) in enumerate(STORES) for c in range(c0, c0 + nch) for k in range(k0, k0 + nk)
-        ]
+        tiles = [(k, c) for k in range(K_TILES) for c in range(CHUNKS)]
         open_banks = {}
 
         def base_pass(i):
-            n, k, c = tiles[i]
-            acc = bank((i + 4) % 8)
+            k, c = tiles[i]
+            acc = bank(i + PACK)
             open_banks[i] = acc
             nc.tensor.matmul_mx(
                 out=acc[:],
@@ -147,10 +137,9 @@ def tile_mix_lrbwd_none_kernel(tc, dy, w4_words, w4_scales, bu, ad, out_0, out_1
                 stop=False,
             )
 
-        def adapter_pass(i):
-            n, k, c = tiles[i]
-            k0, nk, c0, nch = STORES[n]
-            a, g = divmod(k, W // P)
+        def adapter_pass(i, engine):
+            k, c = tiles[i]
+            a, g = divmod(k, HALF // P)
             cols = slice(g * P, (g + 1) * P)
             nc.tensor.matmul_mx(
                 out=open_banks[i][:],
@@ -161,61 +150,41 @@ def tile_mix_lrbwd_none_kernel(tc, dy, w4_words, w4_scales, bu, ad, out_0, out_1
                 start=False,
                 stop=True,
             )
-            engine = "vector" if i == SHARED_ONCE or (i >= SHARED_FROM and i % 2 == 1) else "scalar"
-            copy(engine, dx_sb[n][:, k - k0, (c - c0) * W : (c - c0 + 1) * W], open_banks[i][:])
-            if i + 1 == len(tiles) or tiles[i + 1][0] != n:
-                nc.sync.dma_start(out=dx_out[:, k0 : k0 + nk, c0 * W : (c0 + nch) * W], in_=dx_sb[n][:])
+            copy(engine, dx_sb[k][:, c * W : (c + 1) * W], open_banks[i][:])
+            if c == CHUNKS - 1:
+                nc.sync.dma_start(out=out_0[k * P : (k + 1) * P, :], in_=dx_sb[k][:])
 
-        def open_tiles(first, last):
-            for i in range(first, last):
-                base_pass(i)
-
-        def close_tiles(first, last):
-            for i in range(first, last):
-                adapter_pass(i)
-
+        prepare(dy_q[0], dy_raw[0][:], E5M2)
         bu_interleave("vector", 0, BU_VECTOR)
         bu_interleave("scalar", BU_VECTOR, P)
-        quantize(bu_q, E4M3, 0, HALF)
-        quantize(bu_q, E4M3, HALF, W)
-        interleave("vector", dy_q[0], dy_raw[0][:], 0, HALF)
-        interleave("vector", dy_q[0], dy_raw[0][:], HALF, DY_VECTOR)
-        interleave("scalar", dy_q[0], dy_raw[0][:], DY_VECTOR, W)
-        quantize(dy_q[0], E5M2, 0, HALF)
-        quantize(dy_q[0], E5M2, HALF, W)
-        h_chunk(0, 0, ["scalar"])
-        interleave("scalar", h_q[0], h_sb[0][:], H0_VECTOR, W)
+        for j in range(PACK):
+            quantize(bu_q, E4M3, j * P, (j + 1) * P)
+        h_chunk(0, 0)
         prepare(dy_q[1], dy_raw[1][:], E5M2)
-        h_chunk(1, 0, ["scalar"])
-        open_tiles(0, 6)
-        interleave("scalar", h_q[1], h_sb[1][:], H1_VECTOR, W)
-        interleave("vector", ad_q[0], ad_raw[0][:], 0, HALF)
-        interleave("vector", h_q[0], h_sb[0][:], 0, H0_VECTOR)
-        quantize(ad_q[0], E4M3, 0, HALF)
-        quantize(h_q[0], E5M2, 0, W)
-        close_tiles(0, 2)
-        open_tiles(6, 8)
-        interleave("vector", ad_q[0], ad_raw[0][:], HALF, W)
-        interleave("vector", h_q[1], h_sb[1][:], 0, P)
-        quantize(ad_q[0], E4M3, HALF, W)
-        close_tiles(2, 4)
-        open_tiles(8, 10)
-        interleave("vector", h_q[1], h_sb[1][:], P, H1_VECTOR)
-        interleave("vector", ad_q[1], ad_raw[1][:], 0, P)
-        quantize(h_q[1], E5M2, 0, W)
-        interleave("vector", ad_q[1], ad_raw[1][:], P, HALF)
-        interleave("vector", ad_q[1], ad_raw[1][:], HALF, W)
-        quantize(ad_q[1], E4M3, 0, HALF)
-        quantize(ad_q[1], E4M3, HALF, W)
-        close_tiles(4, 8)
-        open_tiles(10, 12)
+        h_chunk(1, PACK)
+        nc.sync.dma_start(out=h_out[:, :, 0 : 2 * W], in_=h_first[:])
         prepare(dy_q[2], dy_raw[2][:], E5M2)
-        close_tiles(8, 12)
-        open_tiles(12, 16)
-        h_chunk(2, 4, ["scalar", "vector"])
-        prepare(h_q[2], h_sb[2][:], E5M2)
-        close_tiles(12, 16)
-        open_tiles(16, 22)
-        close_tiles(16, 20)
-        open_tiles(22, 24)
-        close_tiles(20, 24)
+        h_chunk(2, 0)
+        nc.sync.dma_start(out=h_out[:, :, 2 * W : T], in_=h_last[:])
+        for i in range(BANKS):
+            base_pass(i)
+        interleave("scalar", h_q[2], h_sb[2], W - H2_SCALAR, W)
+        interleave("vector", h_q[0], h_sb[0], 0, W)
+        interleave("vector", h_q[1], h_sb[1], 0, W)
+        quantize(h_q[0], E5M2, 0, W)
+        quantize(h_q[1], E5M2, 0, W)
+        ad_interleave(0)
+        interleave("vector", h_q[2], h_sb[2], 0, W - H2_SCALAR)
+        quantize(ad_q[0], E4M3, 0, HALF)
+        quantize(h_q[2], E5M2, 0, W)
+        ad_interleave(1)
+        for i in range(len(tiles)):
+            if i >= BANKS:
+                base_pass(i)
+            if i == 2:
+                quantize(ad_q[1], E4M3, 0, HALF)
+            if i in (8, 12):
+                ad_interleave(2 + (i - 8) // 4)
+            if i in (10, 14):
+                quantize(ad_q[2 + (i - 10) // 4], E4M3, 0, HALF)
+            adapter_pass(i, "vector" if i % CHUNKS == 1 else "scalar")

@@ -22,8 +22,9 @@ CHUNKS = T // W
 K_TILES = K // P
 BANKS = 8
 ALIGN = 256
-BU_VECTOR = 80
+BU_VECTOR = 88
 H2_SCALAR = 352
+STORES = [(k, 1, 0, CHUNKS) for k in range(K_TILES)]
 
 
 def tile_mix_lrbwd_none_kernel(tc, dy, w4_words, w4_scales, bu, ad, out_0, out_1):
@@ -45,9 +46,10 @@ def tile_mix_lrbwd_none_kernel(tc, dy, w4_words, w4_scales, bu, ad, out_0, out_1
             else:
                 nc.scalar.copy(out=out, in_=in_)
 
-        def interleave(engine, op, raw, lo, hi):
-            src = raw[:, :, lo:hi].rearrange("p j (c i) -> p c j i", i=4)
-            dst = op[0][:, lo * PACK : hi * PACK].rearrange("p (c i j) -> p c j i", i=4, j=PACK)
+        def interleave(engine, op, lo, raw):
+            width = raw.shape[2]
+            src = raw.rearrange("p j (c i) -> p c j i", i=4)
+            dst = op[0][:, lo * PACK : (lo + width) * PACK].rearrange("p (c i j) -> p c j i", i=4, j=PACK)
             copy(engine, dst, src)
 
         def quantize(op, fmt, lo, hi):
@@ -58,21 +60,21 @@ def tile_mix_lrbwd_none_kernel(tc, dy, w4_words, w4_scales, bu, ad, out_0, out_1
                 in_=grouped[:, lo * PACK : hi * PACK],
             )
 
-        def prepare(op, raw, fmt):
-            interleave("vector", op, raw, 0, HALF)
-            interleave("vector", op, raw, HALF, W)
-            quantize(op, fmt, 0, HALF)
-            quantize(op, fmt, HALF, W)
+        def prepare_dy(c):
+            interleave("vector", dy_q[c], 0, dy_raw[c][:, :, 0:HALF])
+            interleave("vector", dy_q[c], HALF, dy_raw[c][:, :, HALF:W])
+            quantize(dy_q[c], E5M2, 0, HALF)
+            quantize(dy_q[c], E5M2, HALF, W)
 
         def bank(i):
             return ps.tile([P, W], F32, name="acc", tag="bank%d" % (i % BANKS))
 
         dy_v = dy.rearrange("(p j) t -> p j t", j=PACK)
         dy_raw = [sb.tile([P, PACK, W], F32, name="dy_raw%d" % c, align_bytes=ALIGN) for c in range(CHUNKS)]
-        ad_raw = sb.tile([P, PACK, K], F32, align_bytes=ALIGN)
-        bu_raw = sb.tile([P, PACK, R], F32, align_bytes=ALIGN)
-        w4_codes = sb.tile([P, 2 * K], U8, align_bytes=ALIGN)
-        w4_plane = sb.tile([P, K], U8, align_bytes=ALIGN)
+        ad_raw = sb.tile([P, PACK, K], F32, name="ad_raw", align_bytes=ALIGN)
+        bu_raw = sb.tile([P, PACK, R], F32, name="bu_raw", align_bytes=ALIGN)
+        w4_codes = sb.tile([P, 2 * K], U8, name="w4_codes", align_bytes=ALIGN)
+        w4_plane = sb.tile([P, K], U8, name="w4_plane", align_bytes=ALIGN)
 
         nc.gpsimd.memset(w4_plane[:].bitcast(I32), 0)
         for q in range(4):
@@ -91,21 +93,31 @@ def tile_mix_lrbwd_none_kernel(tc, dy, w4_words, w4_scales, bu, ad, out_0, out_1
         h_q = [operand("h%d" % c, W) for c in range(CHUNKS)]
         ad_q = [operand("ad%d" % a, HALF) for a in range(K // HALF)]
         bu_q = operand("bu", R)
-        h_first = sb.tile([P, PACK, 2 * W], F32, align_bytes=ALIGN)
-        h_last = sb.tile([P, PACK, W], F32, align_bytes=ALIGN)
-        h_sb = [h_first[:, :, 0:W], h_first[:, :, W : 2 * W], h_last[:]]
-        dx_sb = [sb.tile([P, T], F32, name="dx_sb%d" % k, align_bytes=ALIGN) for k in range(K_TILES)]
+        h_first = sb.tile([P, PACK, W], F32, name="h_first", align_bytes=ALIGN)
+        h_rest = sb.tile([P, PACK, 2 * W], F32, name="h_rest", align_bytes=ALIGN)
+        h_sb = [h_first[:], h_rest[:, :, 0:W], h_rest[:, :, W : 2 * W]]
         h_out = out_1.rearrange("(p j) t -> p j t", j=PACK)
+        dx_sb = [
+            sb.tile([P, nk, nc_ * W], F32, name="dx_sb%d" % n, align_bytes=ALIGN)
+            for n, (k0, nk, c0, nc_) in enumerate(STORES)
+        ]
+        places = {
+            (k, c): (n, k - k0, c - c0)
+            for n, (k0, nk, c0, nc_) in enumerate(STORES)
+            for k in range(k0, k0 + nk)
+            for c in range(c0, c0 + nc_)
+        }
+        dx_out = out_0.rearrange("(g p) t -> p g t", p=P)
 
         def bu_interleave(engine, lo, hi):
             dst = bu_q[0][:].rearrange("p (s m j) -> p m j s", s=PACK, j=PACK)
             src = bu_raw[:].rearrange("p j (m s) -> p m j s", s=PACK)
             copy(engine, dst[:, lo:hi], src[:, lo:hi])
 
-        def ad_interleave(a):
-            interleave("vector", ad_q[a], ad_raw[:, :, a * HALF : (a + 1) * HALF], 0, HALF)
+        def ad_interleave(a, lo, hi):
+            interleave("vector", ad_q[a], lo, ad_raw[:, :, a * HALF + lo : a * HALF + hi])
 
-        def h_chunk(c, first_bank):
+        def h_chunk(c, first_bank, vector_row=None):
             for j in range(PACK):
                 acc = bank(first_bank + j)
                 cols = slice(j * P, (j + 1) * P)
@@ -118,15 +130,13 @@ def tile_mix_lrbwd_none_kernel(tc, dy, w4_words, w4_scales, bu, ad, out_0, out_1
                     start=True,
                     stop=True,
                 )
-                copy("scalar", h_sb[c][:, j, :], acc[:])
+                copy("vector" if j == vector_row else "scalar", h_sb[c][:, j, :], acc[:])
 
-        tiles = [(k, c) for k in range(K_TILES) for c in range(CHUNKS)]
         open_banks = {}
 
-        def base_pass(i):
-            k, c = tiles[i]
-            acc = bank(i + PACK)
-            open_banks[i] = acc
+        def base_pass(k, c):
+            acc = bank(len(open_banks) + PACK)
+            open_banks[k, c] = acc
             nc.tensor.matmul_mx(
                 out=acc[:],
                 lhsT=w4_codes[:, 2 * k * P : 2 * (k + 1) * P].bitcast(E2M1),
@@ -137,12 +147,11 @@ def tile_mix_lrbwd_none_kernel(tc, dy, w4_words, w4_scales, bu, ad, out_0, out_1
                 stop=False,
             )
 
-        def adapter_pass(i, engine):
-            k, c = tiles[i]
+        def adapter_pass(k, c, engine):
             a, g = divmod(k, HALF // P)
             cols = slice(g * P, (g + 1) * P)
             nc.tensor.matmul_mx(
-                out=open_banks[i][:],
+                out=open_banks[k, c][:],
                 lhsT=ad_q[a][1][:, cols].bitcast(E4M3),
                 lhsT_scale=ad_q[a][2][:, cols],
                 rhs=h_q[c][1][:].bitcast(E5M2),
@@ -150,41 +159,55 @@ def tile_mix_lrbwd_none_kernel(tc, dy, w4_words, w4_scales, bu, ad, out_0, out_1
                 start=False,
                 stop=True,
             )
-            copy(engine, dx_sb[k][:, c * W : (c + 1) * W], open_banks[i][:])
-            if c == CHUNKS - 1:
-                nc.sync.dma_start(out=out_0[k * P : (k + 1) * P, :], in_=dx_sb[k][:])
+            n, g, e = places[k, c]
+            copy(engine, dx_sb[n][:, g, e * W : (e + 1) * W], open_banks[k, c][:])
 
-        prepare(dy_q[0], dy_raw[0][:], E5M2)
+        def store(n):
+            k0, nk, c0, nc_ = STORES[n]
+            nc.sync.dma_start(out=dx_out[:, k0 : k0 + nk, c0 * W : (c0 + nc_) * W], in_=dx_sb[n][:])
+
+        def tile_passes(k, c, engine):
+            base_pass(k, c)
+            adapter_pass(k, c, engine)
+
+        prepare_dy(0)
         bu_interleave("vector", 0, BU_VECTOR)
         bu_interleave("scalar", BU_VECTOR, P)
         for j in range(PACK):
             quantize(bu_q, E4M3, j * P, (j + 1) * P)
         h_chunk(0, 0)
-        prepare(dy_q[1], dy_raw[1][:], E5M2)
+        nc.sync.dma_start(out=h_out[:, :, 0:W], in_=h_first[:])
+        prepare_dy(1)
         h_chunk(1, PACK)
-        nc.sync.dma_start(out=h_out[:, :, 0 : 2 * W], in_=h_first[:])
-        prepare(dy_q[2], dy_raw[2][:], E5M2)
-        h_chunk(2, 0)
-        nc.sync.dma_start(out=h_out[:, :, 2 * W : T], in_=h_last[:])
-        for i in range(BANKS):
-            base_pass(i)
-        interleave("scalar", h_q[2], h_sb[2], W - H2_SCALAR, W)
-        interleave("vector", h_q[0], h_sb[0], 0, W)
-        interleave("vector", h_q[1], h_sb[1], 0, W)
+        prepare_dy(2)
+        interleave("vector", h_q[0], 0, h_sb[0])
+        h_chunk(2, 0, vector_row=1)
+        nc.sync.dma_start(out=h_out[:, :, W:T], in_=h_rest[:])
+        tiles = [(k, c) for c in range(CHUNKS) for k in range(2)]
+        tiles = tiles + [(k, c) for k in range(2, K_TILES) for c in range(CHUNKS)]
+        for k, c in tiles[:BANKS]:
+            base_pass(k, c)
+        interleave("scalar", h_q[2], 0, h_sb[2][:, :, 0:H2_SCALAR])
         quantize(h_q[0], E5M2, 0, W)
+        interleave("vector", h_q[1], 0, h_sb[1])
+        ad_interleave(0, 0, P)
+        ad_interleave(0, P, HALF)
+        quantize(ad_q[0], E4M3, 0, P)
+        quantize(ad_q[0], E4M3, P, HALF)
+        interleave("vector", h_q[2], H2_SCALAR, h_sb[2][:, :, H2_SCALAR:W])
         quantize(h_q[1], E5M2, 0, W)
-        ad_interleave(0)
-        interleave("vector", h_q[2], h_sb[2], 0, W - H2_SCALAR)
-        quantize(ad_q[0], E4M3, 0, HALF)
         quantize(h_q[2], E5M2, 0, W)
-        ad_interleave(1)
-        for i in range(len(tiles)):
+        ad_interleave(1, 0, P)
+        ad_interleave(1, P, HALF)
+        quantize(ad_q[1], E4M3, 0, P)
+        quantize(ad_q[1], E4M3, P, HALF)
+        for i, (k, c) in enumerate(tiles):
             if i >= BANKS:
-                base_pass(i)
-            if i == 2:
-                quantize(ad_q[1], E4M3, 0, HALF)
-            if i in (8, 12):
-                ad_interleave(2 + (i - 8) // 4)
-            if i in (10, 14):
-                quantize(ad_q[2 + (i - 10) // 4], E4M3, 0, HALF)
-            adapter_pass(i, "vector" if i % CHUNKS == 1 else "scalar")
+                base_pass(k, c)
+            adapter_pass(k, c, "vector" if i in (3, 5) or (i > 5 and c == 1) else "scalar")
+            if c == CHUNKS - 1:
+                store(k)
+            if i in (5, 7):
+                ad_interleave(2 + (i - 5) // 2, 0, HALF)
+            if i in (7, 10):
+                quantize(ad_q[2 + (i - 7) // 3], E4M3, 0, HALF)

@@ -23,7 +23,8 @@ K_TILES = K // P
 BANKS = 8
 ALIGN = 256
 BU_VECTOR = 88
-H2_SCALAR = 352
+H2_SCALAR = 416
+EARLY = 7
 STORES = [(k, 1, 0, CHUNKS) for k in range(K_TILES)]
 
 
@@ -183,31 +184,37 @@ def tile_mix_lrbwd_none_kernel(tc, dy, w4_words, w4_scales, bu, ad, out_0, out_1
         interleave("vector", h_q[0], 0, h_sb[0])
         h_chunk(2, 0, vector_row=1)
         nc.sync.dma_start(out=h_out[:, :, W:T], in_=h_rest[:])
-        tiles = [(k, c) for c in range(CHUNKS) for k in range(2)]
-        tiles = tiles + [(k, c) for k in range(2, K_TILES) for c in range(CHUNKS)]
-        for k, c in tiles[:BANKS]:
+        tiles = [(k, c) for k in range(K_TILES) for c in range(CHUNKS)]
+        for k, c in tiles[:EARLY]:
             base_pass(k, c)
         interleave("scalar", h_q[2], 0, h_sb[2][:, :, 0:H2_SCALAR])
         quantize(h_q[0], E5M2, 0, W)
-        interleave("vector", h_q[1], 0, h_sb[1])
+        interleave("vector", h_q[1], 0, h_sb[1][:, :, 0:HALF])
         ad_interleave(0, 0, P)
-        ad_interleave(0, P, HALF)
+        interleave("vector", h_q[1], HALF, h_sb[1][:, :, HALF:W])
         quantize(ad_q[0], E4M3, 0, P)
-        quantize(ad_q[0], E4M3, P, HALF)
         interleave("vector", h_q[2], H2_SCALAR, h_sb[2][:, :, H2_SCALAR:W])
         quantize(h_q[1], E5M2, 0, W)
         quantize(h_q[2], E5M2, 0, W)
+        ad_interleave(0, P, HALF)
         ad_interleave(1, 0, P)
+        quantize(ad_q[0], E4M3, P, HALF)
         ad_interleave(1, P, HALF)
         quantize(ad_q[1], E4M3, 0, P)
         quantize(ad_q[1], E4M3, P, HALF)
-        for i, (k, c) in enumerate(tiles):
-            if i >= BANKS:
-                base_pass(k, c)
-            adapter_pass(k, c, "vector" if i in (3, 5) or (i > 5 and c == 1) else "scalar")
-            if c == CHUNKS - 1:
-                store(k)
-            if i in (5, 7):
-                ad_interleave(2 + (i - 5) // 2, 0, HALF)
-            if i in (7, 10):
-                quantize(ad_q[2 + (i - 7) // 3], E4M3, 0, HALF)
+        for k in range(K_TILES):
+            for c in range(CHUNKS):
+                if (k, c) not in open_banks:
+                    base_pass(k, c)
+            for c in range(CHUNKS):
+                adapter_pass(k, c, "vector" if k > 0 and c == (2 if k == 1 else 1) else "scalar")
+                if (k, c) == (0, 0):
+                    base_pass(*tiles[EARLY])
+            store(k)
+            if k == 0:
+                for later in tiles[BANKS : BANKS + 2]:
+                    base_pass(*later)
+            if k in (1, 2):
+                ad_interleave(k + 1, 0, HALF)
+            if k in (2, 3):
+                quantize(ad_q[k], E4M3, 0, HALF)

from contextlib import ExitStack

import concourse.mybir as mybir

N, R, K, T = 512, 512, 1024, 1536
FLOPS = 2 * N * R * T + 2 * (N + R) * K * T

F32 = mybir.dt.float32
BF16 = mybir.dt.bfloat16
I32 = mybir.dt.int32
U32 = mybir.dt.uint32
U8 = mybir.dt.uint8
E4M3 = mybir.dt.float8_e4m3fn_x4
E5M2 = mybir.dt.float8_e5m2_x4
E2M1 = mybir.dt.float4_e2m1fn_x4

P = 128
PACK = 4
W = 512
HALF = W // 2
CHUNKS = T // W
K_TILES = K // P
BANKS = 8
ALIGN = 256
BU_VECTOR = 88
H2_SCALAR = 416
EARLY = 7
STORES = [(k, 1, 0, CHUNKS) for k in range(K_TILES)]


def tile_mix_lrbwd_none_kernel(tc, dy, w4_words, w4_scales, bu, ad, out_0, out_1):
    nc = tc.nc
    with ExitStack() as ctx:
        sb = ctx.enter_context(tc.tile_pool(name="sb", bufs=1))
        ps = ctx.enter_context(tc.psum_pool(name="ps", bufs=1))
        ctx.enter_context(tc.manual_schedule())

        def operand(name, width):
            grouped = sb.tile([P, width * PACK], BF16, name=name + "_bf", align_bytes=ALIGN)
            codes = sb.tile([P, width], U32, name=name + "_codes", align_bytes=ALIGN)
            scales = sb.tile([P, width], U8, name=name + "_scales", align_bytes=ALIGN)
            return grouped, codes, scales

        def copy(engine, out, in_):
            if engine == "vector":
                nc.vector.tensor_copy(out=out, in_=in_)
            else:
                nc.scalar.copy(out=out, in_=in_)

        def interleave(engine, op, lo, raw):
            width = raw.shape[2]
            src = raw.rearrange("p j (c i) -> p c j i", i=4)
            dst = op[0][:, lo * PACK : (lo + width) * PACK].rearrange("p (c i j) -> p c j i", i=4, j=PACK)
            copy(engine, dst, src)

        def quantize(op, fmt, lo, hi):
            grouped, codes, scales = op
            nc.vector.quantize_mx(
                out=codes[:, lo:hi].bitcast(fmt),
                scales=scales[:, lo:hi],
                in_=grouped[:, lo * PACK : hi * PACK],
            )

        def prepare_dy(c):
            interleave("vector", dy_q[c], 0, dy_raw[c][:, :, 0:HALF])
            interleave("vector", dy_q[c], HALF, dy_raw[c][:, :, HALF:W])
            quantize(dy_q[c], E5M2, 0, HALF)
            quantize(dy_q[c], E5M2, HALF, W)

        def bank(i):
            return ps.tile([P, W], F32, name="acc", tag="bank%d" % (i % BANKS))

        dy_v = dy.rearrange("(p j) t -> p j t", j=PACK)
        dy_raw = [sb.tile([P, PACK, W], F32, name="dy_raw%d" % c, align_bytes=ALIGN) for c in range(CHUNKS)]
        ad_raw = sb.tile([P, PACK, K], F32, name="ad_raw", align_bytes=ALIGN)
        bu_raw = sb.tile([P, PACK, R], F32, name="bu_raw", align_bytes=ALIGN)
        w4_codes = sb.tile([P, 2 * K], U8, name="w4_codes", align_bytes=ALIGN)
        w4_plane = sb.tile([P, K], U8, name="w4_plane", align_bytes=ALIGN)

        nc.gpsimd.memset(w4_plane[:].bitcast(I32), 0)
        for q in range(4):
            nc.gpsimd.dma_start(
                out=w4_plane[32 * q : 32 * q + 4, :].bitcast(I32),
                in_=w4_scales[0, 4 * q : 4 * q + 4, :].bitcast(I32),
            )
        nc.sync.dma_start(out=dy_raw[0][:], in_=dy_v[:, :, 0:W])
        nc.sync.dma_start(out=bu_raw[:], in_=bu.rearrange("(p j) r -> p j r", j=PACK))
        for c in range(1, CHUNKS):
            nc.sync.dma_start(out=dy_raw[c][:], in_=dy_v[:, :, c * W : (c + 1) * W])
        nc.sync.dma_start(out=w4_codes[:].bitcast(I32), in_=w4_words[0].bitcast(I32))
        nc.sync.dma_start(out=ad_raw[:], in_=ad.rearrange("(p j) k -> p j k", j=PACK))

        dy_q = [operand("dy%d" % c, W) for c in range(CHUNKS)]
        h_q = [operand("h%d" % c, W) for c in range(CHUNKS)]
        ad_q = [operand("ad%d" % a, HALF) for a in range(K // HALF)]
        bu_q = operand("bu", R)
        h_first = sb.tile([P, PACK, W], F32, name="h_first", align_bytes=ALIGN)
        h_rest = sb.tile([P, PACK, 2 * W], F32, name="h_rest", align_bytes=ALIGN)
        h_sb = [h_first[:], h_rest[:, :, 0:W], h_rest[:, :, W : 2 * W]]
        h_out = out_1.rearrange("(p j) t -> p j t", j=PACK)
        dx_sb = [
            sb.tile([P, nk, nc_ * W], F32, name="dx_sb%d" % n, align_bytes=ALIGN)
            for n, (k0, nk, c0, nc_) in enumerate(STORES)
        ]
        places = {
            (k, c): (n, k - k0, c - c0)
            for n, (k0, nk, c0, nc_) in enumerate(STORES)
            for k in range(k0, k0 + nk)
            for c in range(c0, c0 + nc_)
        }
        dx_out = out_0.rearrange("(g p) t -> p g t", p=P)

        def bu_interleave(engine, lo, hi):
            dst = bu_q[0][:].rearrange("p (s m j) -> p m j s", s=PACK, j=PACK)
            src = bu_raw[:].rearrange("p j (m s) -> p m j s", s=PACK)
            copy(engine, dst[:, lo:hi], src[:, lo:hi])

        def ad_interleave(a, lo, hi):
            interleave("vector", ad_q[a], lo, ad_raw[:, :, a * HALF + lo : a * HALF + hi])

        def h_chunk(c, first_bank, vector_row=None):
            for j in range(PACK):
                acc = bank(first_bank + j)
                cols = slice(j * P, (j + 1) * P)
                nc.tensor.matmul_mx(
                    out=acc[:],
                    lhsT=bu_q[1][:, cols].bitcast(E4M3),
                    lhsT_scale=bu_q[2][:, cols],
                    rhs=dy_q[c][1][:].bitcast(E5M2),
                    rhs_scale=dy_q[c][2][:],
                    start=True,
                    stop=True,
                )
                copy("vector" if j == vector_row else "scalar", h_sb[c][:, j, :], acc[:])

        open_banks = {}

        def base_pass(k, c):
            acc = bank(len(open_banks) + PACK)
            open_banks[k, c] = acc
            nc.tensor.matmul_mx(
                out=acc[:],
                lhsT=w4_codes[:, 2 * k * P : 2 * (k + 1) * P].bitcast(E2M1),
                lhsT_scale=w4_plane[:, k * P : (k + 1) * P],
                rhs=dy_q[c][1][:].bitcast(E5M2),
                rhs_scale=dy_q[c][2][:],
                start=True,
                stop=False,
            )

        def adapter_pass(k, c, engine):
            a, g = divmod(k, HALF // P)
            cols = slice(g * P, (g + 1) * P)
            nc.tensor.matmul_mx(
                out=open_banks[k, c][:],
                lhsT=ad_q[a][1][:, cols].bitcast(E4M3),
                lhsT_scale=ad_q[a][2][:, cols],
                rhs=h_q[c][1][:].bitcast(E5M2),
                rhs_scale=h_q[c][2][:],
                start=False,
                stop=True,
            )
            n, g, e = places[k, c]
            copy(engine, dx_sb[n][:, g, e * W : (e + 1) * W], open_banks[k, c][:])

        def store(n):
            k0, nk, c0, nc_ = STORES[n]
            nc.sync.dma_start(out=dx_out[:, k0 : k0 + nk, c0 * W : (c0 + nc_) * W], in_=dx_sb[n][:])

        def tile_passes(k, c, engine):
            base_pass(k, c)
            adapter_pass(k, c, engine)

        prepare_dy(0)
        bu_interleave("vector", 0, BU_VECTOR)
        bu_interleave("scalar", BU_VECTOR, P)
        for j in range(PACK):
            quantize(bu_q, E4M3, j * P, (j + 1) * P)
        h_chunk(0, 0)
        nc.sync.dma_start(out=h_out[:, :, 0:W], in_=h_first[:])
        prepare_dy(1)
        h_chunk(1, PACK)
        prepare_dy(2)
        interleave("vector", h_q[0], 0, h_sb[0])
        h_chunk(2, 0, vector_row=1)
        nc.sync.dma_start(out=h_out[:, :, W:T], in_=h_rest[:])
        tiles = [(k, c) for k in range(K_TILES) for c in range(CHUNKS)]
        for k, c in tiles[:EARLY]:
            base_pass(k, c)
        interleave("scalar", h_q[2], 0, h_sb[2][:, :, 0:H2_SCALAR])
        quantize(h_q[0], E5M2, 0, W)
        interleave("vector", h_q[1], 0, h_sb[1][:, :, 0:HALF])
        ad_interleave(0, 0, P)
        interleave("vector", h_q[1], HALF, h_sb[1][:, :, HALF:W])
        quantize(ad_q[0], E4M3, 0, P)
        interleave("vector", h_q[2], H2_SCALAR, h_sb[2][:, :, H2_SCALAR:W])
        quantize(h_q[1], E5M2, 0, W)
        quantize(h_q[2], E5M2, 0, W)
        ad_interleave(0, P, HALF)
        ad_interleave(1, 0, P)
        quantize(ad_q[0], E4M3, P, HALF)
        ad_interleave(1, P, HALF)
        quantize(ad_q[1], E4M3, 0, P)
        quantize(ad_q[1], E4M3, P, HALF)
        for k in range(K_TILES):
            for c in range(CHUNKS):
                if (k, c) not in open_banks:
                    base_pass(k, c)
            for c in range(CHUNKS):
                adapter_pass(k, c, "vector" if k > 0 and c == (2 if k == 1 else 1) else "scalar")
                if (k, c) == (0, 0):
                    base_pass(*tiles[EARLY])
            store(k)
            if k == 0:
                for later in tiles[BANKS : BANKS + 2]:
                    base_pass(*later)
            if k in (1, 2):
                ad_interleave(k + 1, 0, HALF)
            if k in (2, 3):
                quantize(ad_q[k], E4M3, 0, HALF)
